import numpy as np
import ml_dtypes


def mxq(x, axis, fmt="e4m3"):
    dtype, down = {"e4m3": (ml_dtypes.float8_e4m3fn, 7), "e5m2": (ml_dtypes.float8_e5m2, 14)}[fmt]
    v = np.moveaxis(np.asarray(x, np.float32).astype(ml_dtypes.bfloat16).astype(np.float64), axis, -1)
    blocks = v.reshape(v.shape[:-1] + (-1, 32))
    amax = np.abs(blocks).max(-1, keepdims=True)
    byte = np.maximum(np.where(amax > 0, np.frexp(amax)[1] - 1 + 127, 0) - down, 1)
    scale = np.exp2(byte - 127.0)
    codes = (blocks / scale).astype(np.float32).astype(dtype).astype(np.float64)
    return np.moveaxis((codes * scale).reshape(v.shape), -1, axis)


WIDE = False


def mx_kscale(k):
    if not WIDE:
        return np.ones(k)
    levels = np.array([10, -10, 5, -5, 0])
    if k % 512:
        return np.exp2(np.random.permutation(np.resize(levels, k // 32))).repeat(32)
    a = np.empty((k // 512, 16))
    for p in range(k // 512):
        a[p, :8] = np.random.permutation(np.resize(levels, 8))
        for g in range(8):
            far = levels[np.abs(levels - a[p, g]) >= 10]
            a[p, g + 8] = far[np.random.randint(len(far))]
    return np.exp2(a.ravel()).repeat(32)


def f64(x):
    return np.asarray(x).astype(np.float64)


def striped(idx):
    return np.tile(np.asarray(idx).reshape(-1, 16).T, (8, 1)).astype(np.uint16)


def unstriped(offs):
    return offs[:16].T.reshape(-1).astype(np.int64)


def bf(x):
    return np.asarray(x, np.float32).astype(ml_dtypes.bfloat16)


def planes(Y):
    r, m = Y.shape
    b = f64(bf(Y)).reshape(r // 32, 32, m)
    amax = np.abs(b).max(1)
    byte = np.clip(np.where(amax > 0, np.frexp(amax)[1] - 1 + 127 - 7, 1), 1, 254)
    codes = (b * np.exp2(127.0 - byte)[:, None, :]).reshape(r, m).astype(np.float32).astype(ml_dtypes.float8_e4m3fn).view(np.uint8)
    words = codes.reshape(r // 512, 128, 4, m).transpose(0, 1, 3, 2)
    return np.ascontiguousarray(words), np.ascontiguousarray(byte.astype(np.uint8).reshape(r // 512, 16, m))


D, T, I, F = 512, 2048, 512, 512


def setup_inputs():
    n = np.random.standard_normal
    idx = np.sort(np.random.permutation(T)[:I])
    fd = mx_kscale(D)
    return {
        "tok": (n((D, T)) / fd[:, None]).astype(np.float32),
        "fa": (np.random.uniform(0.5, 1.0, (D, 1))).astype(np.float32),
        "fb": (np.random.uniform(-0.5, 0.5, (D, 1))).astype(np.float32),
        "fc": (np.random.uniform(-0.5, 0.5, (D, 1))).astype(np.float32),
        "fe": (np.random.uniform(-0.5, 0.5, (D, 1))).astype(np.float32),
        "wo": (n((D, F)) * 1 / np.sqrt(D) * fd[:, None]).astype(np.float32),
        "offs": striped(idx),
    }


def reference(tok, fa, fb, fc, fe, wo, offs):
    idx = unstriped(offs)
    x1 = np.pad(f64(tok)[:, idx], ((0, 0), (1, 0)))[:, :I]
    x2 = np.pad(f64(tok)[:, idx], ((0, 0), (2, 0)))[:, :I]
    x3 = np.pad(f64(tok)[:, idx], ((0, 0), (3, 0)))[:, :I]
    x = f64(tok)[:, idx] * f64(fa) + x1 * f64(fb) + x2 * f64(fc) + x3 * f64(fe)
    woq = mxq(f64(wo), 0, "e4m3")
    xq = mxq(x, 0, "e4m3")
    y = woq.T @ xq
    words, scales = planes(y)
    return y, words, scales

@@ -1,0 +1,182 @@
+from contextlib import ExitStack
+
+import concourse.mybir as mybir
+
+D, T, I, F = 512, 2048, 512, 512
+FLOPS = 2 * D * F * I
+
+F32 = mybir.dt.float32
+BF16 = mybir.dt.bfloat16
+I32 = mybir.dt.int32
+U32 = mybir.dt.uint32
+U16 = mybir.dt.uint16
+U8 = mybir.dt.uint8
+FP8X4 = mybir.dt.float8_e4m3fn_x4
+MULT = mybir.AluOpType.mult
+ADD = mybir.AluOpType.add
+COPY = mybir.ActivationFunctionType.Copy
+
+P = 128
+PACK = 4
+PAD = 8
+HALF = I // 2
+CHUNK = 128
+RUN = 4
+
+
+def tile_attend_shortconv_pl_kernel(tc, tok, fa, fb, fc, fe, wo, offs, out_0, out_1, out_2):
+    nc = tc.nc
+    tok_planes = tok.rearrange("(p t) n -> p t n", t=PACK)
+    wo_planes = wo.rearrange("(p t) f -> p t f", t=PACK)
+    y_rows = out_0.rearrange("(p r) i -> p r i", r=PACK)
+    words_out = out_1[0].rearrange("p c r -> p (c r)").bitcast(I32)
+    scales_out = out_2[0].bitcast(I32)
+
+    with ExitStack() as ctx:
+        keep = ctx.enter_context(tc.tile_pool(name="keep", bufs=1))
+        psum = ctx.enter_context(tc.psum_pool(name="psum", bufs=1))
+
+        offsets = keep.tile([P, I // 16], U16, name="offsets")
+        pool = [keep.tile([P, T], F32, name=f"pool{t}", align_bytes=64) for t in range(PACK)]
+        taps = [keep.tile([P, PACK], F32, name=f"tap{k}") for k in range(4)]
+        w_raw = [keep.tile([P, PACK, F // 2], F32, name=f"w_raw{h}", align_bytes=64) for h in range(2)]
+        picked = [keep.tile([P, PAD + I], F32, name=f"picked{t}", align_bytes=64) for t in range(PACK)]
+        prod0 = [keep.tile([P, I], F32, name=f"prod0_{t}", align_bytes=64) for t in range(PACK)]
+        prod2 = [keep.tile([P, I], F32, name=f"prod2_{t}", align_bytes=64) for t in range(PACK)]
+        near = keep.tile([P, PACK, I], F32, name="near", align_bytes=64)
+        far = keep.tile([P, PACK, I], F32, name="far", align_bytes=64)
+        zeros = keep.tile([P, PAD], F32, name="zeros")
+        w_bf = keep.tile([P, PACK, P, PACK], BF16, name="w_bf", align_bytes=64)
+        w_codes = keep.tile([P, F], U32, name="w_codes", align_bytes=64)
+        w_scales = keep.tile([P, F], U8, name="w_scales", align_bytes=64)
+        y_codes = keep.tile([P, I], U32, name="y_codes", align_bytes=64)
+        y_scales = keep.tile([P, I], U8, name="y_scales", align_bytes=64)
+
+        nc.sync.dma_start(offsets[:], offs)
+        nc.sync.dma_start(pool[0][:], tok_planes[:, 0, :])
+        for k, factor in enumerate((fa, fb, fc, fe)):
+            nc.sync.dma_start(taps[k][:], factor.rearrange("(p t) o -> p (t o)", t=PACK))
+        nc.sync.dma_start(pool[1][:], tok_planes[:, 1, :])
+        nc.sync.dma_start(pool[2][:], tok_planes[:, 2, :])
+        nc.sync.dma_start(w_raw[0][:], wo_planes[:, :, 0 : F // 2])
+        nc.sync.dma_start(pool[3][:], tok_planes[:, 3, :])
+        nc.sync.dma_start(w_raw[1][:], wo_planes[:, :, F // 2 : F])
+
+        nc.vector.memset(zeros[:], 0.0)
+        for t in range(PACK):
+            nc.scalar.activation(picked[t][:, 0:PAD], zeros[:], COPY)
+
+        def shifted(t, k, lo, hi):
+            return picked[t][:, PAD + lo - k : PAD + hi - k]
+
+        def tap(k, t):
+            return taps[k][:, t : t + 1]
+
+        def mix_plane(t):
+            for lo in (0, HALF):
+                hi = lo + HALF
+                nc.vector.tensor_copy(shifted(t, 0, lo, hi), pool[t][:].indirect(offsets[:, lo // 16 : hi // 16]))
+            for lo in (0, HALF):
+                hi = lo + HALF
+                nc.scalar.activation(prod0[t][:, lo:hi], shifted(t, 0, lo, hi), COPY, scale=tap(0, t))
+                nc.scalar.activation(prod2[t][:, lo:hi], shifted(t, 2, lo, hi), COPY, scale=tap(2, t))
+            for lo in (0, HALF):
+                hi = lo + HALF
+                nc.vector.scalar_tensor_tensor(near[:, t, lo:hi], shifted(t, 1, lo, hi), tap(1, t), prod0[t][:, lo:hi], MULT, ADD)
+                nc.vector.scalar_tensor_tensor(far[:, t, lo:hi], shifted(t, 3, lo, hi), tap(3, t), prod2[t][:, lo:hi], MULT, ADD)
+
+        def round_w(h):
+            m = slice(h * P // 2, (h + 1) * P // 2)
+            nc.scalar.copy(
+                w_bf[:, :, m, :].rearrange("p r m t -> p m t r"),
+                w_raw[h][:].rearrange("p t (m r) -> p m t r", r=PACK),
+            )
+
+        def interleaved(tile_bf):
+            return tile_bf[:].rearrange("p (c i) t -> p c t i", i=RUN)
+
+        def runs(planes):
+            return planes.rearrange("p t (c i) -> p c t i", i=RUN)
+
+        x_bf, x_codes, x_scales, acc, y_sb, y_bf = [], [], [], [], [], []
+        for c in range(I // CHUNK):
+            x_bf.append(keep.tile([P, CHUNK, PACK], BF16, name=f"x_bf{c}", align_bytes=64))
+            x_codes.append(keep.tile([P, CHUNK], U32, name=f"x_codes{c}", align_bytes=64))
+            x_scales.append(keep.tile([P, CHUNK], U8, name=f"x_scales{c}", align_bytes=64))
+            acc.append(psum.tile([P, PACK, CHUNK], F32, name=f"acc{c}"))
+            y_sb.append(keep.tile([P, PACK, CHUNK], F32, name=f"y_sb{c}", align_bytes=64))
+            y_bf.append(keep.tile([P, CHUNK, PACK], BF16, name=f"y_bf{c}", align_bytes=64))
+
+        def slots(c):
+            return slice(c * CHUNK, (c + 1) * CHUNK)
+
+        def finish_x(c):
+            nc.vector.tensor_tensor(interleaved(x_bf[c]), runs(near[:, :, slots(c)]), runs(far[:, :, slots(c)]), ADD)
+
+        def quantize_x(c):
+            nc.vector.quantize_mx(
+                out=x_codes[c][:].bitcast(FP8X4), scales=x_scales[c][:], in_=x_bf[c][:].rearrange("p i t -> p (i t)")
+            )
+
+        def project(c):
+            for r in range(PACK):
+                cols = slice(r * P, (r + 1) * P)
+                nc.tensor.matmul_mx(
+                    out=acc[c][:, r, :],
+                    lhsT=w_codes[:, cols].bitcast(FP8X4),
+                    lhsT_scale=w_scales[:, cols],
+                    rhs=x_codes[c][:].bitcast(FP8X4),
+                    rhs_scale=x_scales[c][:],
+                    start=True,
+                    stop=True,
+                )
+            nc.scalar.copy(y_sb[c][:], acc[c][:])
+            nc.sync.dma_start(y_rows[:, :, slots(c)], y_sb[c][:])
+
+        def round_y(c):
+            if c < 2:
+                nc.scalar.copy(y_bf[c][:], acc[c][:].rearrange("p r i -> p i r"))
+            else:
+                nc.vector.tensor_copy(interleaved(y_bf[c]), runs(y_sb[c][:]))
+
+        def quantize_y(c):
+            nc.vector.quantize_mx(
+                out=y_codes[:, slots(c)].bitcast(FP8X4),
+                scales=y_scales[:, slots(c)],
+                in_=y_bf[c][:].rearrange("p i r -> p (i r)"),
+            )
+
+        mix_plane(0)
+        mix_plane(1)
+        mix_plane(2)
+        round_w(0)
+        mix_plane(3)
+        round_w(1)
+        finish_x(0)
+        finish_x(1)
+        quantize_x(0)
+        nc.vector.quantize_mx(
+            out=w_codes[:].bitcast(FP8X4), scales=w_scales[:], in_=w_bf[:].rearrange("p r m t -> p (r m t)")
+        )
+        project(0)
+        round_y(0)
+        quantize_x(1)
+        finish_x(2)
+        project(1)
+        round_y(1)
+        finish_x(3)
+        quantize_x(2)
+        project(2)
+        quantize_x(3)
+        project(3)
+        quantize_y(0)
+        quantize_y(1)
+        nc.sync.dma_start(words_out[:, 0:HALF], y_codes[:, 0:HALF].bitcast(I32))
+        round_y(2)
+        round_y(3)
+        quantize_y(2)
+        quantize_y(3)
+        nc.sync.dma_start(words_out[:, HALF:I], y_codes[:, HALF:I].bitcast(I32))
+        for q in range(4):
+            queue = nc.sync if q % 2 == 0 else nc.scalar
+            queue.dma_start(scales_out[4 * q : 4 * q + 4, :], y_scales[32 * q : 32 * q + 4, :].bitcast(I32))

@@ -22,6 +22,7 @@ PAD = 8
 HALF = I // 2
 CHUNK = 128
 RUN = 4
+PREFIX = T - HALF
 
 
 def tile_attend_shortconv_pl_kernel(tc, tok, fa, fb, fc, fe, wo, offs, out_0, out_1, out_2):
@@ -53,13 +54,15 @@ def tile_attend_shortconv_pl_kernel(tc, tok, fa, fb, fc, fe, wo, offs, out_0, ou
         y_scales = keep.tile([P, I], U8, name="y_scales", align_bytes=64)
 
         nc.sync.dma_start(offsets[:], offs)
-        nc.sync.dma_start(pool[0][:], tok_planes[:, 0, :])
-        for k, factor in enumerate((fa, fb, fc, fe)):
+        nc.sync.dma_start(pool[0][:, 0:PREFIX], tok_planes[:, 0, 0:PREFIX])
+        nc.sync.dma_start(pool[0][:, PREFIX:T], tok_planes[:, 0, PREFIX:T])
+        for k, factor in ((0, fa), (2, fc), (1, fb), (3, fe)):
             nc.sync.dma_start(taps[k][:], factor.rearrange("(p t) o -> p (t o)", t=PACK))
         nc.sync.dma_start(pool[1][:], tok_planes[:, 1, :])
         nc.sync.dma_start(pool[2][:], tok_planes[:, 2, :])
         nc.sync.dma_start(w_raw[0][:], wo_planes[:, :, 0 : F // 2])
-        nc.sync.dma_start(pool[3][:], tok_planes[:, 3, :])
+        nc.sync.dma_start(pool[3][:, 0:PREFIX], tok_planes[:, 3, 0:PREFIX])
+        nc.sync.dma_start(pool[3][:, PREFIX:T], tok_planes[:, 3, PREFIX:T])
         nc.sync.dma_start(w_raw[1][:], wo_planes[:, :, F // 2 : F])
 
         nc.vector.memset(zeros[:], 0.0)
@@ -72,18 +75,27 @@ def tile_attend_shortconv_pl_kernel(tc, tok, fa, fb, fc, fe, wo, offs, out_0, ou
         def tap(k, t):
             return taps[k][:, t : t + 1]
 
-        def mix_plane(t):
-            for lo in (0, HALF):
-                hi = lo + HALF
-                nc.vector.tensor_copy(shifted(t, 0, lo, hi), pool[t][:].indirect(offsets[:, lo // 16 : hi // 16]))
+        def gather(t):
+            nc.vector.tensor_copy(shifted(t, 0, 0, HALF), pool[t][:, 0:PREFIX].indirect(offsets[:, 0 : HALF // 16]))
+            nc.vector.tensor_copy(shifted(t, 0, HALF, I), pool[t][:].indirect(offsets[:, HALF // 16 : I // 16]))
             for lo in (0, HALF):
                 hi = lo + HALF
                 nc.scalar.activation(prod0[t][:, lo:hi], shifted(t, 0, lo, hi), COPY, scale=tap(0, t))
                 nc.scalar.activation(prod2[t][:, lo:hi], shifted(t, 2, lo, hi), COPY, scale=tap(2, t))
+
+        def mix_near(t, lo):
+            hi = lo + HALF
+            nc.vector.scalar_tensor_tensor(near[:, t, lo:hi], shifted(t, 1, lo, hi), tap(1, t), prod0[t][:, lo:hi], MULT, ADD)
+
+        def mix_far(t, lo):
+            hi = lo + HALF
+            nc.vector.scalar_tensor_tensor(far[:, t, lo:hi], shifted(t, 3, lo, hi), tap(3, t), prod2[t][:, lo:hi], MULT, ADD)
+
+        def mix_plane(t):
+            gather(t)
             for lo in (0, HALF):
-                hi = lo + HALF
-                nc.vector.scalar_tensor_tensor(near[:, t, lo:hi], shifted(t, 1, lo, hi), tap(1, t), prod0[t][:, lo:hi], MULT, ADD)
-                nc.vector.scalar_tensor_tensor(far[:, t, lo:hi], shifted(t, 3, lo, hi), tap(3, t), prod2[t][:, lo:hi], MULT, ADD)
+                mix_near(t, lo)
+                mix_far(t, lo)
 
         def round_w(h):
             m = slice(h * P // 2, (h + 1) * P // 2)
@@ -98,12 +110,11 @@ def tile_attend_shortconv_pl_kernel(tc, tok, fa, fb, fc, fe, wo, offs, out_0, ou
         def runs(planes):
             return planes.rearrange("p t (c i) -> p c t i", i=RUN)
 
-        x_bf, x_codes, x_scales, acc, y_sb, y_bf = [], [], [], [], [], []
+        x_bf, x_codes, x_scales, y_sb, y_bf = [], [], [], [], []
         for c in range(I // CHUNK):
             x_bf.append(keep.tile([P, CHUNK, PACK], BF16, name=f"x_bf{c}", align_bytes=64))
             x_codes.append(keep.tile([P, CHUNK], U32, name=f"x_codes{c}", align_bytes=64))
             x_scales.append(keep.tile([P, CHUNK], U8, name=f"x_scales{c}", align_bytes=64))
-            acc.append(psum.tile([P, PACK, CHUNK], F32, name=f"acc{c}"))
             y_sb.append(keep.tile([P, PACK, CHUNK], F32, name=f"y_sb{c}", align_bytes=64))
             y_bf.append(keep.tile([P, CHUNK, PACK], BF16, name=f"y_bf{c}", align_bytes=64))
 
@@ -118,65 +129,76 @@ def tile_attend_shortconv_pl_kernel(tc, tok, fa, fb, fc, fe, wo, offs, out_0, ou
                 out=x_codes[c][:].bitcast(FP8X4), scales=x_scales[c][:], in_=x_bf[c][:].rearrange("p i t -> p (i t)")
             )
 
-        def project(c):
-            for r in range(PACK):
-                cols = slice(r * P, (r + 1) * P)
-                nc.tensor.matmul_mx(
-                    out=acc[c][:, r, :],
-                    lhsT=w_codes[:, cols].bitcast(FP8X4),
-                    lhsT_scale=w_scales[:, cols],
-                    rhs=x_codes[c][:].bitcast(FP8X4),
-                    rhs_scale=x_scales[c][:],
-                    start=True,
-                    stop=True,
-                )
-            nc.scalar.copy(y_sb[c][:], acc[c][:])
+        def project(c, banks):
+            per_bank = PACK // banks
+            for b in range(banks):
+                acc = psum.tile([P, per_bank, CHUNK], F32, name=f"acc{c}_{b}")
+                for j in range(per_bank):
+                    r = b * per_bank + j
+                    cols = slice(r * P, (r + 1) * P)
+                    nc.tensor.matmul_mx(
+                        out=acc[:, j, :],
+                        lhsT=w_codes[:, cols].bitcast(FP8X4),
+                        lhsT_scale=w_scales[:, cols],
+                        rhs=x_codes[c][:].bitcast(FP8X4),
+                        rhs_scale=x_scales[c][:],
+                        start=True,
+                        stop=True,
+                    )
+                nc.scalar.copy(y_sb[c][:, b * per_bank : (b + 1) * per_bank, :], acc[:])
             nc.sync.dma_start(y_rows[:, :, slots(c)], y_sb[c][:])
 
-        def round_y(c):
-            if c < 2:
-                nc.scalar.copy(y_bf[c][:], acc[c][:].rearrange("p r i -> p i r"))
-            else:
-                nc.vector.tensor_copy(interleaved(y_bf[c]), runs(y_sb[c][:]))
+        def round_y(c, lo, hi):
+            nc.vector.tensor_copy(
+                y_bf[c][:, lo:hi, :].rearrange("p (c i) r -> p c r i", i=RUN), runs(y_sb[c][:, :, lo:hi])
+            )
 
-        def quantize_y(c):
+        def quantize_y(c, lo, hi):
+            cols = slice(c * CHUNK + lo, c * CHUNK + hi)
             nc.vector.quantize_mx(
-                out=y_codes[:, slots(c)].bitcast(FP8X4),
-                scales=y_scales[:, slots(c)],
-                in_=y_bf[c][:].rearrange("p i r -> p (i r)"),
+                out=y_codes[:, cols].bitcast(FP8X4),
+                scales=y_scales[:, cols],
+                in_=y_bf[c][:, lo:hi, :].rearrange("p i r -> p (i r)"),
             )
 
         mix_plane(0)
         mix_plane(1)
         mix_plane(2)
         round_w(0)
-        mix_plane(3)
+        gather(3)
         round_w(1)
+        mix_near(3, 0)
+        mix_far(3, 0)
+        mix_near(3, HALF)
         finish_x(0)
-        finish_x(1)
-        quantize_x(0)
         nc.vector.quantize_mx(
             out=w_codes[:].bitcast(FP8X4), scales=w_scales[:], in_=w_bf[:].rearrange("p r m t -> p (r m t)")
         )
-        project(0)
-        round_y(0)
-        quantize_x(1)
+        quantize_x(0)
+        project(0, 1)
+        mix_far(3, HALF)
+        finish_x(1)
         finish_x(2)
-        project(1)
-        round_y(1)
+        quantize_x(1)
+        project(1, 1)
         finish_x(3)
         quantize_x(2)
-        project(2)
+        project(2, 1)
         quantize_x(3)
-        project(3)
-        quantize_y(0)
-        quantize_y(1)
-        nc.sync.dma_start(words_out[:, 0:HALF], y_codes[:, 0:HALF].bitcast(I32))
-        round_y(2)
-        round_y(3)
-        quantize_y(2)
-        quantize_y(3)
-        nc.sync.dma_start(words_out[:, HALF:I], y_codes[:, HALF:I].bitcast(I32))
+        project(3, PACK)
+        round_y(0, 0, CHUNK)
+        round_y(1, 0, CHUNK)
+        quantize_y(0, 0, CHUNK)
+        quantize_y(1, 0, CHUNK)
+        round_y(2, 0, CHUNK)
+        quantize_y(2, 0, CHUNK)
+        last = I - CHUNK
+        nc.sync.dma_start(words_out[:, 0:last], y_codes[:, 0:last].bitcast(I32))
+        round_y(3, 0, CHUNK // 2)
+        round_y(3, CHUNK // 2, CHUNK)
+        quantize_y(3, 0, CHUNK // 2)
+        quantize_y(3, CHUNK // 2, CHUNK)
+        nc.sync.dma_start(words_out[:, last:I], y_codes[:, last:I].bitcast(I32))
         for q in range(4):
             queue = nc.sync if q % 2 == 0 else nc.scalar
             queue.dma_start(scales_out[4 * q : 4 * q + 4, :], y_scales[32 * q : 32 * q + 4, :].bitcast(I32))

@@ -1,6 +1,7 @@
 from contextlib import ExitStack
 
 import concourse.mybir as mybir
+from concourse.masks import make_identity
 
 D, T, I, F = 512, 2048, 512, 512
 FLOPS = 2 * D * F * I
@@ -18,9 +19,11 @@ COPY = mybir.ActivationFunctionType.Copy
 
 P = 128
 PACK = 4
+TAPS = 4
 PAD = 8
 HALF = I // 2
 CHUNK = 128
+CHUNKS = I // CHUNK
 RUN = 4
 PREFIX = T - HALF
 
@@ -39,14 +42,12 @@ def tile_attend_shortconv_pl_kernel(tc, tok, fa, fb, fc, fe, wo, offs, out_0, ou
 
         offsets = keep.tile([P, I // 16], U16, name="offsets")
         pool = [keep.tile([P, T], F32, name=f"pool{t}", align_bytes=64) for t in range(PACK)]
-        taps = [keep.tile([P, PACK], F32, name=f"tap{k}") for k in range(4)]
+        taps = [keep.tile([P, PACK], F32, name=f"tap{k}") for k in range(TAPS)]
         w_raw = [keep.tile([P, PACK, F // 2], F32, name=f"w_raw{h}", align_bytes=64) for h in range(2)]
         picked = [keep.tile([P, PAD + I], F32, name=f"picked{t}", align_bytes=64) for t in range(PACK)]
-        prod0 = [keep.tile([P, I], F32, name=f"prod0_{t}", align_bytes=64) for t in range(PACK)]
-        prod2 = [keep.tile([P, I], F32, name=f"prod2_{t}", align_bytes=64) for t in range(PACK)]
-        near = keep.tile([P, PACK, I], F32, name="near", align_bytes=64)
-        far = keep.tile([P, PACK, I], F32, name="far", align_bytes=64)
+        terms = [[keep.tile([P, I], F32, name=f"term{t}_{k}", align_bytes=64) for k in range(TAPS)] for t in range(PACK)]
         zeros = keep.tile([P, PAD], F32, name="zeros")
+        ident = keep.tile([P, P], F32, name="ident", align_bytes=64)
         w_bf = keep.tile([P, PACK, P, PACK], BF16, name="w_bf", align_bytes=64)
         w_codes = keep.tile([P, F], U32, name="w_codes", align_bytes=64)
         w_scales = keep.tile([P, F], U8, name="w_scales", align_bytes=64)
@@ -60,14 +61,15 @@ def tile_attend_shortconv_pl_kernel(tc, tok, fa, fb, fc, fe, wo, offs, out_0, ou
             nc.sync.dma_start(taps[k][:], factor.rearrange("(p t) o -> p (t o)", t=PACK))
         nc.sync.dma_start(pool[1][:], tok_planes[:, 1, :])
         nc.sync.dma_start(pool[2][:], tok_planes[:, 2, :])
-        nc.sync.dma_start(w_raw[0][:], wo_planes[:, :, 0 : F // 2])
         nc.sync.dma_start(pool[3][:, 0:PREFIX], tok_planes[:, 3, 0:PREFIX])
         nc.sync.dma_start(pool[3][:, PREFIX:T], tok_planes[:, 3, PREFIX:T])
-        nc.sync.dma_start(w_raw[1][:], wo_planes[:, :, F // 2 : F])
+        for h in range(2):
+            nc.sync.dma_start(w_raw[h][:], wo_planes[:, :, h * F // 2 : (h + 1) * F // 2])
 
         nc.vector.memset(zeros[:], 0.0)
         for t in range(PACK):
             nc.scalar.activation(picked[t][:, 0:PAD], zeros[:], COPY)
+        make_identity(nc, ident[:])
 
         def shifted(t, k, lo, hi):
             return picked[t][:, PAD + lo - k : PAD + hi - k]
@@ -75,129 +77,120 @@ def tile_attend_shortconv_pl_kernel(tc, tok, fa, fb, fc, fe, wo, offs, out_0, ou
         def tap(k, t):
             return taps[k][:, t : t + 1]
 
-        def gather(t):
-            nc.vector.tensor_copy(shifted(t, 0, 0, HALF), pool[t][:, 0:PREFIX].indirect(offsets[:, 0 : HALF // 16]))
-            nc.vector.tensor_copy(shifted(t, 0, HALF, I), pool[t][:].indirect(offsets[:, HALF // 16 : I // 16]))
-            for lo in (0, HALF):
-                hi = lo + HALF
-                nc.scalar.activation(prod0[t][:, lo:hi], shifted(t, 0, lo, hi), COPY, scale=tap(0, t))
-                nc.scalar.activation(prod2[t][:, lo:hi], shifted(t, 2, lo, hi), COPY, scale=tap(2, t))
+        def slots(c):
+            return slice(c * CHUNK, (c + 1) * CHUNK)
 
-        def mix_near(t, lo):
-            hi = lo + HALF
-            nc.vector.scalar_tensor_tensor(near[:, t, lo:hi], shifted(t, 1, lo, hi), tap(1, t), prod0[t][:, lo:hi], MULT, ADD)
+        def gather(t, lo, hi):
+            window = pool[t][:, 0 : T - I + hi]
+            nc.vector.tensor_copy(shifted(t, 0, lo, hi), window.indirect(offsets[:, lo // 16 : hi // 16]))
+            for k in range(TAPS):
+                if k % 2 == 0:
+                    nc.scalar.activation(terms[t][k][:, lo:hi], shifted(t, k, lo, hi), COPY, scale=tap(k, t))
+                else:
+                    nc.vector.tensor_scalar(terms[t][k][:, lo:hi], shifted(t, k, lo, hi), tap(k, t), None, MULT)
 
-        def mix_far(t, lo):
-            hi = lo + HALF
-            nc.vector.scalar_tensor_tensor(far[:, t, lo:hi], shifted(t, 3, lo, hi), tap(3, t), prod2[t][:, lo:hi], MULT, ADD)
+        sums = [psum.tile([P, PACK, P], F32, name=f"sums{c}", tag=f"bank{c}") for c in range(CHUNKS)]
+        back = [psum.tile([P, 2, CHUNK], F32, name=f"back{c}") for c in range(CHUNKS)]
+        pairs = [[keep.tile([P, P, 2], BF16, name=f"pairs{c}_{u}", align_bytes=64) for u in range(2)] for c in range(CHUNKS)]
 
-        def mix_plane(t):
-            gather(t)
-            for lo in (0, HALF):
-                mix_near(t, lo)
-                mix_far(t, lo)
+        def add_terms(t, c):
+            order = (1, 3, 0, 2)
+            for j, k in enumerate(order):
+                nc.tensor.matmul(
+                    sums[c][:, t, :], terms[t][k][:, slots(c)], ident[:], start=j == 0, stop=j == TAPS - 1, is_transpose=True
+                )
+
+        def round_x(c, u):
+            nc.scalar.copy(pairs[c][u][:], sums[c][:, 2 * u : 2 * u + 2, :].rearrange("i e p -> i p e"))
+
+        def turn_back(c, u):
+            words = pairs[c][u][:].rearrange("i p e -> i (p e)").bitcast(F32)
+            nc.tensor.transpose(back[c][:, u, :], words, ident[:])
 
         def round_w(h):
             m = slice(h * P // 2, (h + 1) * P // 2)
-            nc.scalar.copy(
+            nc.vector.tensor_copy(
                 w_bf[:, :, m, :].rearrange("p r m t -> p m t r"),
                 w_raw[h][:].rearrange("p t (m r) -> p m t r", r=PACK),
             )
-
-        def interleaved(tile_bf):
-            return tile_bf[:].rearrange("p (c i) t -> p c t i", i=RUN)
 
         def runs(planes):
             return planes.rearrange("p t (c i) -> p c t i", i=RUN)
 
         x_bf, x_codes, x_scales, y_sb, y_bf = [], [], [], [], []
-        for c in range(I // CHUNK):
-            x_bf.append(keep.tile([P, CHUNK, PACK], BF16, name=f"x_bf{c}", align_bytes=64))
+        for c in range(CHUNKS):
+            x_bf.append(keep.tile([P, CHUNK, 2], F32, name=f"x_bf{c}", align_bytes=64))
             x_codes.append(keep.tile([P, CHUNK], U32, name=f"x_codes{c}", align_bytes=64))
             x_scales.append(keep.tile([P, CHUNK], U8, name=f"x_scales{c}", align_bytes=64))
             y_sb.append(keep.tile([P, PACK, CHUNK], F32, name=f"y_sb{c}", align_bytes=64))
             y_bf.append(keep.tile([P, CHUNK, PACK], BF16, name=f"y_bf{c}", align_bytes=64))
 
-        def slots(c):
-            return slice(c * CHUNK, (c + 1) * CHUNK)
-
-        def finish_x(c):
-            nc.vector.tensor_tensor(interleaved(x_bf[c]), runs(near[:, :, slots(c)]), runs(far[:, :, slots(c)]), ADD)
+        def weave_x(c):
+            nc.scalar.copy(x_bf[c][:], back[c][:].rearrange("p u i -> p i u"))
 
         def quantize_x(c):
             nc.vector.quantize_mx(
-                out=x_codes[c][:].bitcast(FP8X4), scales=x_scales[c][:], in_=x_bf[c][:].rearrange("p i t -> p (i t)")
+                out=x_codes[c][:].bitcast(FP8X4),
+                scales=x_scales[c][:],
+                in_=x_bf[c][:].rearrange("p i u -> p (i u)").bitcast(BF16),
             )
 
-        def project(c, banks):
-            per_bank = PACK // banks
-            for b in range(banks):
-                acc = psum.tile([P, per_bank, CHUNK], F32, name=f"acc{c}_{b}")
-                for j in range(per_bank):
-                    r = b * per_bank + j
-                    cols = slice(r * P, (r + 1) * P)
-                    nc.tensor.matmul_mx(
-                        out=acc[:, j, :],
-                        lhsT=w_codes[:, cols].bitcast(FP8X4),
-                        lhsT_scale=w_scales[:, cols],
-                        rhs=x_codes[c][:].bitcast(FP8X4),
-                        rhs_scale=x_scales[c][:],
-                        start=True,
-                        stop=True,
-                    )
-                nc.scalar.copy(y_sb[c][:, b * per_bank : (b + 1) * per_bank, :], acc[:])
+        def project(c):
+            acc = psum.tile([P, PACK, CHUNK], F32, name=f"acc{c}", tag=f"bank{c}")
+            for r in range(PACK):
+                cols = slice(r * P, (r + 1) * P)
+                nc.tensor.matmul_mx(
+                    out=acc[:, r, :],
+                    lhsT=w_codes[:, cols].bitcast(FP8X4),
+                    lhsT_scale=w_scales[:, cols],
+                    rhs=x_codes[c][:].bitcast(FP8X4),
+                    rhs_scale=x_scales[c][:],
+                    start=True,
+                    stop=True,
+                )
+            nc.scalar.copy(y_sb[c][:], acc[:])
             nc.sync.dma_start(y_rows[:, :, slots(c)], y_sb[c][:])
 
-        def round_y(c, lo, hi):
-            nc.vector.tensor_copy(
-                y_bf[c][:, lo:hi, :].rearrange("p (c i) r -> p c r i", i=RUN), runs(y_sb[c][:, :, lo:hi])
-            )
+        def round_y(c):
+            nc.vector.tensor_copy(y_bf[c][:].rearrange("p (c i) r -> p c r i", i=RUN), runs(y_sb[c][:]))
 
-        def quantize_y(c, lo, hi):
-            cols = slice(c * CHUNK + lo, c * CHUNK + hi)
+        def quantize_y(c):
             nc.vector.quantize_mx(
-                out=y_codes[:, cols].bitcast(FP8X4),
-                scales=y_scales[:, cols],
-                in_=y_bf[c][:, lo:hi, :].rearrange("p i r -> p (i r)"),
+                out=y_codes[:, slots(c)].bitcast(FP8X4),
+                scales=y_scales[:, slots(c)],
+                in_=y_bf[c][:].rearrange("p i r -> p (i r)"),
             )
 
-        mix_plane(0)
-        mix_plane(1)
-        mix_plane(2)
+        for t in range(PACK):
+            cuts = (0, HALF, I) if t in (0, PACK - 1) else (0, I)
+            for lo, hi in zip(cuts, cuts[1:]):
+                gather(t, lo, hi)
+            for c in range(CHUNKS):
+                add_terms(t, c)
+                if t % 2 == 1:
+                    round_x(c, t // 2)
+            if t % 2 == 1:
+                for c in range(CHUNKS):
+                    turn_back(c, t // 2)
         round_w(0)
-        gather(3)
         round_w(1)
-        mix_near(3, 0)
-        mix_far(3, 0)
-        mix_near(3, HALF)
-        finish_x(0)
+        for c in range(CHUNKS):
+            weave_x(c)
+        quantize_x(0)
         nc.vector.quantize_mx(
             out=w_codes[:].bitcast(FP8X4), scales=w_scales[:], in_=w_bf[:].rearrange("p r m t -> p (r m t)")
         )
-        quantize_x(0)
-        project(0, 1)
-        mix_far(3, HALF)
-        finish_x(1)
-        finish_x(2)
-        quantize_x(1)
-        project(1, 1)
-        finish_x(3)
-        quantize_x(2)
-        project(2, 1)
-        quantize_x(3)
-        project(3, PACK)
-        round_y(0, 0, CHUNK)
-        round_y(1, 0, CHUNK)
-        quantize_y(0, 0, CHUNK)
-        quantize_y(1, 0, CHUNK)
-        round_y(2, 0, CHUNK)
-        quantize_y(2, 0, CHUNK)
+        for c in range(1, CHUNKS):
+            quantize_x(c)
+        for c in range(CHUNKS):
+            project(c)
+        for c in range(CHUNKS):
+            round_y(c)
+            if c > 0:
+                quantize_y(c - 1)
         last = I - CHUNK
         nc.sync.dma_start(words_out[:, 0:last], y_codes[:, 0:last].bitcast(I32))
-        round_y(3, 0, CHUNK // 2)
-        round_y(3, CHUNK // 2, CHUNK)
-        quantize_y(3, 0, CHUNK // 2)
-        quantize_y(3, CHUNK // 2, CHUNK)
+        quantize_y(CHUNKS - 1)
         nc.sync.dma_start(words_out[:, last:I], y_codes[:, last:I].bitcast(I32))
         for q in range(4):
             queue = nc.sync if q % 2 == 0 else nc.scalar

@@ -20,6 +20,7 @@ COPY = mybir.ActivationFunctionType.Copy
 P = 128
 PACK = 4
 TAPS = 4
+TERMS = 3
 PAD = 8
 HALF = I // 2
 CHUNK = 128
@@ -43,9 +44,12 @@ def tile_attend_shortconv_pl_kernel(tc, tok, fa, fb, fc, fe, wo, offs, out_0, ou
         offsets = keep.tile([P, I // 16], U16, name="offsets")
         pool = [keep.tile([P, T], F32, name=f"pool{t}", align_bytes=64) for t in range(PACK)]
         taps = [keep.tile([P, PACK], F32, name=f"tap{k}") for k in range(TAPS)]
-        w_raw = [keep.tile([P, PACK, F // 2], F32, name=f"w_raw{h}", align_bytes=64) for h in range(2)]
+        w_cuts = (0, F // 2, 3 * F // 4, F)
+        w_parts = list(zip(w_cuts, w_cuts[1:]))
+        w_raw = [keep.tile([P, PACK, hi - lo], F32, name=f"w_raw{lo}", align_bytes=64) for lo, hi in w_parts]
         picked = [keep.tile([P, PAD + I], F32, name=f"picked{t}", align_bytes=64) for t in range(PACK)]
-        terms = [[keep.tile([P, I], F32, name=f"term{t}_{k}", align_bytes=64) for k in range(TAPS)] for t in range(PACK)]
+        own = [keep.tile([P, I], F32, name=f"own{t}", align_bytes=64) for t in range(PACK)]
+        terms = [[keep.tile([P, I], F32, name=f"term{t}_{k}", align_bytes=64) for k in range(TERMS)] for t in range(PACK)]
         zeros = keep.tile([P, PAD], F32, name="zeros")
         ident = keep.tile([P, P], F32, name="ident", align_bytes=64)
         w_bf = keep.tile([P, PACK, P, PACK], BF16, name="w_bf", align_bytes=64)
@@ -57,14 +61,14 @@ def tile_attend_shortconv_pl_kernel(tc, tok, fa, fb, fc, fe, wo, offs, out_0, ou
         nc.sync.dma_start(offsets[:], offs)
         nc.sync.dma_start(pool[0][:, 0:PREFIX], tok_planes[:, 0, 0:PREFIX])
         nc.sync.dma_start(pool[0][:, PREFIX:T], tok_planes[:, 0, PREFIX:T])
-        for k, factor in ((0, fa), (2, fc), (1, fb), (3, fe)):
+        for k, factor in ((2, fc), (0, fa), (3, fe), (1, fb)):
             nc.sync.dma_start(taps[k][:], factor.rearrange("(p t) o -> p (t o)", t=PACK))
         nc.sync.dma_start(pool[1][:], tok_planes[:, 1, :])
         nc.sync.dma_start(pool[2][:], tok_planes[:, 2, :])
         nc.sync.dma_start(pool[3][:, 0:PREFIX], tok_planes[:, 3, 0:PREFIX])
         nc.sync.dma_start(pool[3][:, PREFIX:T], tok_planes[:, 3, PREFIX:T])
-        for h in range(2):
-            nc.sync.dma_start(w_raw[h][:], wo_planes[:, :, h * F // 2 : (h + 1) * F // 2])
+        for h, (lo, hi) in enumerate(w_parts):
+            nc.sync.dma_start(w_raw[h][:], wo_planes[:, :, lo:hi])
 
         nc.vector.memset(zeros[:], 0.0)
         for t in range(PACK):
@@ -83,21 +87,23 @@ def tile_attend_shortconv_pl_kernel(tc, tok, fa, fb, fc, fe, wo, offs, out_0, ou
         def gather(t, lo, hi):
             window = pool[t][:, 0 : T - I + hi]
             nc.vector.tensor_copy(shifted(t, 0, lo, hi), window.indirect(offsets[:, lo // 16 : hi // 16]))
-            for k in range(TAPS):
-                if k % 2 == 0:
-                    nc.scalar.activation(terms[t][k][:, lo:hi], shifted(t, k, lo, hi), COPY, scale=tap(k, t))
-                else:
-                    nc.vector.tensor_scalar(terms[t][k][:, lo:hi], shifted(t, k, lo, hi), tap(k, t), None, MULT)
+            nc.scalar.activation(terms[t][0][:, lo:hi], shifted(t, 2, lo, hi), COPY, scale=tap(2, t))
+            nc.scalar.activation(terms[t][1][:, lo:hi], shifted(t, 3, lo, hi), COPY, scale=tap(3, t))
+
+        def scale_own(t, lo, hi):
+            nc.vector.tensor_scalar(own[t][:, lo:hi], shifted(t, 0, lo, hi), tap(0, t), None, MULT)
+
+        def mix(t, lo, hi):
+            nc.vector.scalar_tensor_tensor(terms[t][2][:, lo:hi], shifted(t, 1, lo, hi), tap(1, t), own[t][:, lo:hi], MULT, ADD)
 
         sums = [psum.tile([P, PACK, P], F32, name=f"sums{c}", tag=f"bank{c}") for c in range(CHUNKS)]
-        back = [psum.tile([P, 2, CHUNK], F32, name=f"back{c}") for c in range(CHUNKS)]
+        back = [psum.tile([P, 2, CHUNK], F32, name=f"back{c}", tag=f"bank{CHUNKS + c}") for c in range(CHUNKS)]
         pairs = [[keep.tile([P, P, 2], BF16, name=f"pairs{c}_{u}", align_bytes=64) for u in range(2)] for c in range(CHUNKS)]
 
         def add_terms(t, c):
-            order = (1, 3, 0, 2)
-            for j, k in enumerate(order):
+            for k in range(TERMS):
                 nc.tensor.matmul(
-                    sums[c][:, t, :], terms[t][k][:, slots(c)], ident[:], start=j == 0, stop=j == TAPS - 1, is_transpose=True
+                    sums[c][:, t, :], terms[t][k][:, slots(c)], ident[:], start=k == 0, stop=k == TERMS - 1, is_transpose=True
                 )
 
         def round_x(c, u):
@@ -108,7 +114,7 @@ def tile_attend_shortconv_pl_kernel(tc, tok, fa, fb, fc, fe, wo, offs, out_0, ou
             nc.tensor.transpose(back[c][:, u, :], words, ident[:])
 
         def round_w(h):
-            m = slice(h * P // 2, (h + 1) * P // 2)
+            m = slice(w_parts[h][0] // PACK, w_parts[h][1] // PACK)
             nc.vector.tensor_copy(
                 w_bf[:, :, m, :].rearrange("p r m t -> p m t r"),
                 w_raw[h][:].rearrange("p t (m r) -> p m t r", r=PACK),
@@ -135,20 +141,22 @@ def tile_attend_shortconv_pl_kernel(tc, tok, fa, fb, fc, fe, wo, offs, out_0, ou
                 in_=x_bf[c][:].rearrange("p i u -> p (i u)").bitcast(BF16),
             )
 
-        def project(c):
-            acc = psum.tile([P, PACK, CHUNK], F32, name=f"acc{c}", tag=f"bank{c}")
-            for r in range(PACK):
-                cols = slice(r * P, (r + 1) * P)
-                nc.tensor.matmul_mx(
-                    out=acc[:, r, :],
-                    lhsT=w_codes[:, cols].bitcast(FP8X4),
-                    lhsT_scale=w_scales[:, cols],
-                    rhs=x_codes[c][:].bitcast(FP8X4),
-                    rhs_scale=x_scales[c][:],
-                    start=True,
-                    stop=True,
-                )
-            nc.scalar.copy(y_sb[c][:], acc[:])
+        def project(c, banks):
+            per_bank = PACK // len(banks)
+            for b, bank in enumerate(banks):
+                acc = psum.tile([P, per_bank, CHUNK], F32, name=f"acc{c}_{b}", tag=f"bank{bank}")
+                for j in range(per_bank):
+                    cols = slice((b * per_bank + j) * P, (b * per_bank + j + 1) * P)
+                    nc.tensor.matmul_mx(
+                        out=acc[:, j, :],
+                        lhsT=w_codes[:, cols].bitcast(FP8X4),
+                        lhsT_scale=w_scales[:, cols],
+                        rhs=x_codes[c][:].bitcast(FP8X4),
+                        rhs_scale=x_scales[c][:],
+                        start=True,
+                        stop=True,
+                    )
+                nc.scalar.copy(y_sb[c][:, b * per_bank : (b + 1) * per_bank, :], acc[:])
             nc.sync.dma_start(y_rows[:, :, slots(c)], y_sb[c][:])
 
         def round_y(c):
@@ -162,9 +170,9 @@ def tile_attend_shortconv_pl_kernel(tc, tok, fa, fb, fc, fe, wo, offs, out_0, ou
             )
 
         for t in range(PACK):
-            cuts = (0, HALF, I) if t in (0, PACK - 1) else (0, I)
-            for lo, hi in zip(cuts, cuts[1:]):
-                gather(t, lo, hi)
+            for step in (gather, scale_own, mix):
+                step(t, 0, HALF)
+                step(t, HALF, I)
             for c in range(CHUNKS):
                 add_terms(t, c)
                 if t % 2 == 1:
@@ -172,18 +180,18 @@ def tile_attend_shortconv_pl_kernel(tc, tok, fa, fb, fc, fe, wo, offs, out_0, ou
             if t % 2 == 1:
                 for c in range(CHUNKS):
                     turn_back(c, t // 2)
-        round_w(0)
-        round_w(1)
+        for h in range(len(w_parts)):
+            round_w(h)
         for c in range(CHUNKS):
             weave_x(c)
-        quantize_x(0)
         nc.vector.quantize_mx(
             out=w_codes[:].bitcast(FP8X4), scales=w_scales[:], in_=w_bf[:].rearrange("p r m t -> p (r m t)")
         )
-        for c in range(1, CHUNKS):
-            quantize_x(c)
         for c in range(CHUNKS):
-            project(c)
+            quantize_x(c)
+        for c in range(CHUNKS - 1):
+            project(c, [c])
+        project(CHUNKS - 1, [CHUNKS - 1, CHUNKS])
         for c in range(CHUNKS):
             round_y(c)
             if c > 0:

@@ -46,7 +46,7 @@ def tile_attend_shortconv_pl_kernel(tc, tok, fa, fb, fc, fe, wo, offs, out_0, ou
         taps = [keep.tile([P, PACK], F32, name=f"tap{k}") for k in range(TAPS)]
         w_cuts = (0, F // 2, 3 * F // 4, F)
         w_parts = list(zip(w_cuts, w_cuts[1:]))
-        w_raw = [keep.tile([P, PACK, hi - lo], F32, name=f"w_raw{lo}", align_bytes=64) for lo, hi in w_parts]
+        w_raw = [keep.tile([P, PACK, hi - lo], F32, name=f"w_raw{lo}", tag=f"w_raw{hi}", align_bytes=64) for lo, hi in w_parts]
         picked = [keep.tile([P, PAD + I], F32, name=f"picked{t}", align_bytes=64) for t in range(PACK)]
         own = [keep.tile([P, I], F32, name=f"own{t}", align_bytes=64) for t in range(PACK)]
         terms = [[keep.tile([P, I], F32, name=f"term{t}_{k}", align_bytes=64) for k in range(TERMS)] for t in range(PACK)]
@@ -58,8 +58,8 @@ def tile_attend_shortconv_pl_kernel(tc, tok, fa, fb, fc, fe, wo, offs, out_0, ou
         y_codes = keep.tile([P, I], U32, name="y_codes", align_bytes=64)
         y_scales = keep.tile([P, I], U8, name="y_scales", align_bytes=64)
 
-        nc.sync.dma_start(offsets[:], offs)
         nc.sync.dma_start(pool[0][:, 0:PREFIX], tok_planes[:, 0, 0:PREFIX])
+        nc.sync.dma_start(offsets[:], offs)
         nc.sync.dma_start(pool[0][:, PREFIX:T], tok_planes[:, 0, PREFIX:T])
         for k, factor in ((2, fc), (0, fa), (3, fe), (1, fb)):
             nc.sync.dma_start(taps[k][:], factor.rearrange("(p t) o -> p (t o)", t=PACK))
@@ -94,20 +94,28 @@ def tile_attend_shortconv_pl_kernel(tc, tok, fa, fb, fc, fe, wo, offs, out_0, ou
             nc.vector.tensor_scalar(own[t][:, lo:hi], shifted(t, 0, lo, hi), tap(0, t), None, MULT)
 
         def mix(t, lo, hi):
-            nc.vector.scalar_tensor_tensor(terms[t][2][:, lo:hi], shifted(t, 1, lo, hi), tap(1, t), own[t][:, lo:hi], MULT, ADD)
+            if t == 3 and lo > 0:
+                nc.vector.tensor_scalar(terms[t][2][:, lo:hi], shifted(t, 1, lo, hi), tap(1, t), None, MULT)
+            else:
+                nc.vector.scalar_tensor_tensor(terms[t][2][:, lo:hi], shifted(t, 1, lo, hi), tap(1, t), own[t][:, lo:hi], MULT, ADD)
 
-        sums = [psum.tile([P, PACK, P], F32, name=f"sums{c}", tag=f"bank{c}") for c in range(CHUNKS)]
-        back = [psum.tile([P, 2, CHUNK], F32, name=f"back{c}", tag=f"bank{CHUNKS + c}") for c in range(CHUNKS)]
+        early = [psum.tile([P, 2, 2, P], F32, name=f"early{c}", tag=f"bank{CHUNKS + c}") for c in range(CHUNKS)]
+        late = [psum.tile([P, 2, P], F32, name=f"late{c}", tag=f"bank{c}") for c in range(CHUNKS)]
+        sums = [(early[c][:, 0, :, :], late[c][:]) for c in range(CHUNKS)]
+        back = [early[c][:, 1, :, :] for c in range(CHUNKS)]
         pairs = [[keep.tile([P, P, 2], BF16, name=f"pairs{c}_{u}", align_bytes=64) for u in range(2)] for c in range(CHUNKS)]
 
-        def add_terms(t, c):
-            for k in range(TERMS):
-                nc.tensor.matmul(
-                    sums[c][:, t, :], terms[t][k][:, slots(c)], ident[:], start=k == 0, stop=k == TERMS - 1, is_transpose=True
-                )
+        def add_terms(t, chunks):
+            lo = chunks[0] * CHUNK
+            parts = [own[t], terms[t][0], terms[t][2], terms[t][1]] if t == 3 and lo > 0 else terms[t]
+            for k, part in enumerate(parts):
+                for c in chunks:
+                    nc.tensor.matmul(
+                        sums[c][t // 2][:, t % 2, :], part[:, slots(c)], ident[:], start=k == 0, stop=k == len(parts) - 1, is_transpose=True
+                    )
 
         def round_x(c, u):
-            nc.scalar.copy(pairs[c][u][:], sums[c][:, 2 * u : 2 * u + 2, :].rearrange("i e p -> i p e"))
+            nc.scalar.copy(pairs[c][u][:], sums[c][u].rearrange("i e p -> i p e"))
 
         def turn_back(c, u):
             words = pairs[c][u][:].rearrange("i p e -> i (p e)").bitcast(F32)
@@ -120,23 +128,31 @@ def tile_attend_shortconv_pl_kernel(tc, tok, fa, fb, fc, fe, wo, offs, out_0, ou
                 w_raw[h][:].rearrange("p t (m r) -> p m t r", r=PACK),
             )
 
+        def quantize_w(b):
+            cols = slice(2 * b * P, 2 * (b + 1) * P)
+            nc.vector.quantize_mx(
+                out=w_codes[:, cols].bitcast(FP8X4),
+                scales=w_scales[:, cols],
+                in_=w_bf[:, 2 * b : 2 * b + 2, :, :].rearrange("p r m t -> p (r m t)"),
+            )
+
         def runs(planes):
             return planes.rearrange("p t (c i) -> p c t i", i=RUN)
 
-        x_bf, x_codes, x_scales, y_sb, y_bf = [], [], [], [], []
+        x_codes = keep.tile([P, I], U32, name="x_codes", tag=f"w_raw{F}", align_bytes=64)
+        y_bf = keep.tile([P, I, PACK], BF16, name="y_bf", align_bytes=64)
+        x_bf, x_scales, y_sb = [], [], []
         for c in range(CHUNKS):
             x_bf.append(keep.tile([P, CHUNK, 2], F32, name=f"x_bf{c}", align_bytes=64))
-            x_codes.append(keep.tile([P, CHUNK], U32, name=f"x_codes{c}", align_bytes=64))
             x_scales.append(keep.tile([P, CHUNK], U8, name=f"x_scales{c}", align_bytes=64))
             y_sb.append(keep.tile([P, PACK, CHUNK], F32, name=f"y_sb{c}", align_bytes=64))
-            y_bf.append(keep.tile([P, CHUNK, PACK], BF16, name=f"y_bf{c}", align_bytes=64))
 
         def weave_x(c):
-            nc.scalar.copy(x_bf[c][:], back[c][:].rearrange("p u i -> p i u"))
+            nc.scalar.copy(x_bf[c][:], back[c].rearrange("p u i -> p i u"))
 
         def quantize_x(c):
             nc.vector.quantize_mx(
-                out=x_codes[c][:].bitcast(FP8X4),
+                out=x_codes[:, slots(c)].bitcast(FP8X4),
                 scales=x_scales[c][:],
                 in_=x_bf[c][:].rearrange("p i u -> p (i u)").bitcast(BF16),
             )
@@ -151,55 +167,71 @@ def tile_attend_shortconv_pl_kernel(tc, tok, fa, fb, fc, fe, wo, offs, out_0, ou
                         out=acc[:, j, :],
                         lhsT=w_codes[:, cols].bitcast(FP8X4),
                         lhsT_scale=w_scales[:, cols],
-                        rhs=x_codes[c][:].bitcast(FP8X4),
+                        rhs=x_codes[:, slots(c)].bitcast(FP8X4),
                         rhs_scale=x_scales[c][:],
                         start=True,
                         stop=True,
                     )
                 nc.scalar.copy(y_sb[c][:, b * per_bank : (b + 1) * per_bank, :], acc[:])
-            nc.sync.dma_start(y_rows[:, :, slots(c)], y_sb[c][:])
+                if c == 0:
+                    rows = slice(b * per_bank, (b + 1) * per_bank)
+                    nc.sync.dma_start(y_rows[:, rows, slots(c)], y_sb[c][:, rows, :])
+            if c > 0:
+                nc.sync.dma_start(y_rows[:, :, slots(c)], y_sb[c][:])
 
-        def round_y(c):
-            nc.vector.tensor_copy(y_bf[c][:].rearrange("p (c i) r -> p c r i", i=RUN), runs(y_sb[c][:]))
+        def round_y(lo, hi):
+            c, at = divmod(lo, CHUNK)
+            copy = nc.scalar.copy if hi == I else nc.vector.tensor_copy
+            copy(
+                y_bf[:, lo:hi, :].rearrange("p (c i) r -> p c r i", i=RUN), runs(y_sb[c][:, :, at : at + hi - lo])
+            )
 
-        def quantize_y(c):
+        def quantize_y(lo, hi):
             nc.vector.quantize_mx(
-                out=y_codes[:, slots(c)].bitcast(FP8X4),
-                scales=y_scales[:, slots(c)],
-                in_=y_bf[c][:].rearrange("p i r -> p (i r)"),
+                out=y_codes[:, lo:hi].bitcast(FP8X4),
+                scales=y_scales[:, lo:hi],
+                in_=y_bf[:, lo:hi, :].rearrange("p i r -> p (i r)"),
             )
 
         for t in range(PACK):
             for step in (gather, scale_own, mix):
                 step(t, 0, HALF)
                 step(t, HALF, I)
-            for c in range(CHUNKS):
-                add_terms(t, c)
+            for chunks in ((0, 1), (2, 3)):
+                add_terms(t, chunks)
                 if t % 2 == 1:
-                    round_x(c, t // 2)
-            if t % 2 == 1:
-                for c in range(CHUNKS):
-                    turn_back(c, t // 2)
+                    for c in chunks:
+                        round_x(c, t // 2)
+                    for c in chunks:
+                        turn_back(c, t // 2)
+                if t == PACK - 1 and chunks[0] == 0:
+                    weave_x(0)
         for h in range(len(w_parts)):
             round_w(h)
-        for c in range(CHUNKS):
+        for c in range(1, CHUNKS):
             weave_x(c)
-        nc.vector.quantize_mx(
-            out=w_codes[:].bitcast(FP8X4), scales=w_scales[:], in_=w_bf[:].rearrange("p r m t -> p (r m t)")
-        )
-        for c in range(CHUNKS):
+        quantize_w(0)
+        quantize_x(0)
+        quantize_w(1)
+        for c in range(1, CHUNKS):
             quantize_x(c)
-        for c in range(CHUNKS - 1):
-            project(c, [c])
-        project(CHUNKS - 1, [CHUNKS - 1, CHUNKS])
-        for c in range(CHUNKS):
-            round_y(c)
-            if c > 0:
-                quantize_y(c - 1)
+        project(0, [0, 4])
+        project(1, [1, 5])
+        project(2, [2, 6])
+        project(3, [3, 7, 0, 4])
         last = I - CHUNK
-        nc.sync.dma_start(words_out[:, 0:last], y_codes[:, 0:last].bitcast(I32))
-        quantize_y(CHUNKS - 1)
-        nc.sync.dma_start(words_out[:, last:I], y_codes[:, last:I].bitcast(I32))
+        end = I - CHUNK // 2
+        round_y(0, CHUNK)
+        round_y(CHUNK, HALF)
+        round_y(HALF, last)
+        quantize_y(0, HALF)
+        nc.sync.dma_start(words_out[:, 0:HALF], y_codes[:, 0:HALF].bitcast(I32))
+        round_y(last, end)
+        round_y(end, I)
+        quantize_y(HALF, last)
+        quantize_y(last, end)
+        quantize_y(end, I)
+        nc.sync.dma_start(words_out[:, HALF:I], y_codes[:, HALF:I].bitcast(I32))
         for q in range(4):
             queue = nc.sync if q % 2 == 0 else nc.scalar
             queue.dma_start(scales_out[4 * q : 4 * q + 4, :], y_scales[32 * q : 32 * q + 4, :].bitcast(I32))

@@ -199,26 +199,23 @@ def tile_attend_shortconv_pl_kernel(tc, tok, fa, fb, fc, fe, wo, offs, out_0, ou
                 step(t, HALF, I)
             for chunks in ((0, 1), (2, 3)):
                 add_terms(t, chunks)
-                if t % 2 == 1:
-                    for c in chunks:
-                        round_x(c, t // 2)
-                    for c in chunks:
-                        turn_back(c, t // 2)
-                if t == PACK - 1 and chunks[0] == 0:
-                    weave_x(0)
+            if t >= 2:
+                for step in (round_x, turn_back):
+                    for c in range(CHUNKS):
+                        step(c, t - 2)
         for h in range(len(w_parts)):
             round_w(h)
-        for c in range(1, CHUNKS):
+        for c in range(CHUNKS):
             weave_x(c)
         quantize_w(0)
         quantize_x(0)
         quantize_w(1)
         for c in range(1, CHUNKS):
             quantize_x(c)
-        project(0, [0, 4])
-        project(1, [1, 5])
-        project(2, [2, 6])
-        project(3, [3, 7, 0, 4])
+        project(0, [3, 4])
+        project(1, [0, 5])
+        project(2, [1, 6])
+        project(3, [2, 7, 3, 4])
         last = I - CHUNK
         end = I - CHUNK // 2
         round_y(0, CHUNK)

@@ -94,7 +94,7 @@ def tile_attend_shortconv_pl_kernel(tc, tok, fa, fb, fc, fe, wo, offs, out_0, ou
             nc.vector.tensor_scalar(own[t][:, lo:hi], shifted(t, 0, lo, hi), tap(0, t), None, MULT)
 
         def mix(t, lo, hi):
-            if t == 3 and lo > 0:
+            if t <= 1 or t == 3 and lo > 0:
                 nc.vector.tensor_scalar(terms[t][2][:, lo:hi], shifted(t, 1, lo, hi), tap(1, t), None, MULT)
             else:
                 nc.vector.scalar_tensor_tensor(terms[t][2][:, lo:hi], shifted(t, 1, lo, hi), tap(1, t), own[t][:, lo:hi], MULT, ADD)
@@ -107,7 +107,7 @@ def tile_attend_shortconv_pl_kernel(tc, tok, fa, fb, fc, fe, wo, offs, out_0, ou
 
         def add_terms(t, chunks):
             lo = chunks[0] * CHUNK
-            parts = [own[t], terms[t][0], terms[t][2], terms[t][1]] if t == 3 and lo > 0 else terms[t]
+            parts = [own[t], terms[t][0], terms[t][2], terms[t][1]] if t <= 1 or t == 3 and lo > 0 else terms[t]
             for k, part in enumerate(parts):
                 for c in chunks:
                     nc.tensor.matmul(
@@ -173,10 +173,10 @@ def tile_attend_shortconv_pl_kernel(tc, tok, fa, fb, fc, fe, wo, offs, out_0, ou
                         stop=True,
                     )
                 nc.scalar.copy(y_sb[c][:, b * per_bank : (b + 1) * per_bank, :], acc[:])
-                if c == 0:
+                if c < 2:
                     rows = slice(b * per_bank, (b + 1) * per_bank)
                     nc.sync.dma_start(y_rows[:, rows, slots(c)], y_sb[c][:, rows, :])
-            if c > 0:
+            if c >= 2:
                 nc.sync.dma_start(y_rows[:, :, slots(c)], y_sb[c][:])
 
         def round_y(lo, hi):
@@ -215,7 +215,7 @@ def tile_attend_shortconv_pl_kernel(tc, tok, fa, fb, fc, fe, wo, offs, out_0, ou
         project(0, [3, 4])
         project(1, [0, 5])
         project(2, [1, 6])
-        project(3, [2, 7, 3, 4])
+        project(3, [2, 7])
         last = I - CHUNK
         end = I - CHUNK // 2
         round_y(0, CHUNK)

@@ -141,11 +141,12 @@ def tile_attend_shortconv_pl_kernel(tc, tok, fa, fb, fc, fe, wo, offs, out_0, ou
 
         x_codes = keep.tile([P, I], U32, name="x_codes", tag=f"w_raw{F}", align_bytes=64)
         y_bf = keep.tile([P, I, PACK], BF16, name="y_bf", align_bytes=64)
-        x_bf, x_scales, y_sb = [], [], []
+        y_all = keep.tile([P, PACK, I], F32, name="y_all", align_bytes=64)
+        y_sb = [y_all[:, :, slots(c)] for c in range(CHUNKS)]
+        x_bf, x_scales = [], []
         for c in range(CHUNKS):
             x_bf.append(keep.tile([P, CHUNK, 2], F32, name=f"x_bf{c}", align_bytes=64))
             x_scales.append(keep.tile([P, CHUNK], U8, name=f"x_scales{c}", align_bytes=64))
-            y_sb.append(keep.tile([P, PACK, CHUNK], F32, name=f"y_sb{c}", align_bytes=64))
 
         def weave_x(c):
             nc.scalar.copy(x_bf[c][:], back[c].rearrange("p u i -> p i u"))
@@ -157,27 +158,23 @@ def tile_attend_shortconv_pl_kernel(tc, tok, fa, fb, fc, fe, wo, offs, out_0, ou
                 in_=x_bf[c][:].rearrange("p i u -> p (i u)").bitcast(BF16),
             )
 
-        def project(c, banks):
-            per_bank = PACK // len(banks)
-            for b, bank in enumerate(banks):
-                acc = psum.tile([P, per_bank, CHUNK], F32, name=f"acc{c}_{b}", tag=f"bank{bank}")
-                for j in range(per_bank):
-                    cols = slice((b * per_bank + j) * P, (b * per_bank + j + 1) * P)
-                    nc.tensor.matmul_mx(
-                        out=acc[:, j, :],
-                        lhsT=w_codes[:, cols].bitcast(FP8X4),
-                        lhsT_scale=w_scales[:, cols],
-                        rhs=x_codes[:, slots(c)].bitcast(FP8X4),
-                        rhs_scale=x_scales[c][:],
-                        start=True,
-                        stop=True,
-                    )
-                nc.scalar.copy(y_sb[c][:, b * per_bank : (b + 1) * per_bank, :], acc[:])
-                if c < 2:
-                    rows = slice(b * per_bank, (b + 1) * per_bank)
-                    nc.sync.dma_start(y_rows[:, rows, slots(c)], y_sb[c][:, rows, :])
-            if c >= 2:
-                nc.sync.dma_start(y_rows[:, :, slots(c)], y_sb[c][:])
+        def project(c, b, bank):
+            acc = psum.tile([P, 2, CHUNK], F32, name=f"acc{c}_{b}", tag=f"bank{bank}")
+            for j in range(2):
+                cols = slice((2 * b + j) * P, (2 * b + j + 1) * P)
+                nc.tensor.matmul_mx(
+                    out=acc[:, j, :],
+                    lhsT=w_codes[:, cols].bitcast(FP8X4),
+                    lhsT_scale=w_scales[:, cols],
+                    rhs=x_codes[:, slots(c)].bitcast(FP8X4),
+                    rhs_scale=x_scales[c][:],
+                    start=True,
+                    stop=True,
+                )
+            nc.scalar.copy(y_sb[c][:, 2 * b : 2 * b + 2, :], acc[:])
+
+        def store_y(b, lo, hi):
+            nc.sync.dma_start(y_rows[:, 2 * b : 2 * b + 2, lo:hi], y_all[:, 2 * b : 2 * b + 2, lo:hi])
 
         def round_y(lo, hi):
             c, at = divmod(lo, CHUNK)
@@ -212,10 +209,12 @@ def tile_attend_shortconv_pl_kernel(tc, tok, fa, fb, fc, fe, wo, offs, out_0, ou
         quantize_w(1)
         for c in range(1, CHUNKS):
             quantize_x(c)
-        project(0, [3, 4])
-        project(1, [0, 5])
-        project(2, [1, 6])
-        project(3, [2, 7])
+        banks = (3, 0, 4, 5, 1, 2, 6, 7)
+        for h in range(2):
+            for b in range(2):
+                for c in (2 * h, 2 * h + 1):
+                    project(c, b, banks[4 * h + 2 * b + c % 2])
+                store_y(b, h * HALF, (h + 1) * HALF)
         last = I - CHUNK
         end = I - CHUNK // 2
         round_y(0, CHUNK)

@@ -39,34 +39,45 @@ def tile_attend_shortconv_pl_kernel(tc, tok, fa, fb, fc, fe, wo, offs, out_0, ou
 
     with ExitStack() as ctx:
         keep = ctx.enter_context(tc.tile_pool(name="keep", bufs=1))
+        shared = ctx.enter_context(tc.tile_pool(name="shared", bufs=1))
         psum = ctx.enter_context(tc.psum_pool(name="psum", bufs=1))
 
         offsets = keep.tile([P, I // 16], U16, name="offsets")
-        pool = [keep.tile([P, T], F32, name=f"pool{t}", align_bytes=64) for t in range(PACK)]
+        pool = [keep.tile([P, T], F32, name=f"pool{t}", tag=f"pool{t}", align_bytes=64) for t in range(PACK)]
         taps = [keep.tile([P, PACK], F32, name=f"tap{k}") for k in range(TAPS)]
-        w_cuts = (0, F // 2, 3 * F // 4, F)
+        w_cuts = (0, F // 4, 11 * F // 16, F)
         w_parts = list(zip(w_cuts, w_cuts[1:]))
-        w_raw = [keep.tile([P, PACK, hi - lo], F32, name=f"w_raw{lo}", tag=f"w_raw{hi}", align_bytes=64) for lo, hi in w_parts]
+        w_raw = [keep.tile([P, PACK, hi - lo], F32, name=f"w_raw{lo}", align_bytes=64) for lo, hi in w_parts[:-1]]
+        w_raw.append(shared.tile([P, PACK, F - w_cuts[-2]], F32, name="w_last", align_bytes=64, offset=0))
         picked = [keep.tile([P, PAD + I], F32, name=f"picked{t}", align_bytes=64) for t in range(PACK)]
-        own = [keep.tile([P, I], F32, name=f"own{t}", align_bytes=64) for t in range(PACK)]
-        terms = [[keep.tile([P, I], F32, name=f"term{t}_{k}", align_bytes=64) for k in range(TERMS)] for t in range(PACK)]
+        terms = [
+            [
+                [keep.tile([P, HALF], F32, name=f"term{t}_{h}_{k}", tag=f"term{1 if (t, h) == (2, 0) else t}_{h}_{k}", align_bytes=64) for k in range(TERMS)]
+                for h in range(2)
+            ]
+            for t in range(PACK)
+        ]
         zeros = keep.tile([P, PAD], F32, name="zeros")
         ident = keep.tile([P, P], F32, name="ident", align_bytes=64)
         w_bf = keep.tile([P, PACK, P, PACK], BF16, name="w_bf", align_bytes=64)
         w_codes = keep.tile([P, F], U32, name="w_codes", align_bytes=64)
         w_scales = keep.tile([P, F], U8, name="w_scales", align_bytes=64)
+        y_all = keep.tile([P, PACK, I], F32, name="y_all", align_bytes=64)
+        y_bf = keep.tile([P, I, PACK], BF16, name="y_bf", align_bytes=64)
         y_codes = keep.tile([P, I], U32, name="y_codes", align_bytes=64)
         y_scales = keep.tile([P, I], U8, name="y_scales", align_bytes=64)
 
         nc.sync.dma_start(pool[0][:, 0:PREFIX], tok_planes[:, 0, 0:PREFIX])
         nc.sync.dma_start(offsets[:], offs)
-        nc.sync.dma_start(pool[0][:, PREFIX:T], tok_planes[:, 0, PREFIX:T])
-        for k, factor in ((2, fc), (0, fa), (3, fe), (1, fb)):
+        for k, factor in ((2, fc), (0, fa), (1, fb), (3, fe)):
             nc.sync.dma_start(taps[k][:], factor.rearrange("(p t) o -> p (t o)", t=PACK))
-        nc.sync.dma_start(pool[1][:], tok_planes[:, 1, :])
-        nc.sync.dma_start(pool[2][:], tok_planes[:, 2, :])
-        nc.sync.dma_start(pool[3][:, 0:PREFIX], tok_planes[:, 3, 0:PREFIX])
-        nc.sync.dma_start(pool[3][:, PREFIX:T], tok_planes[:, 3, PREFIX:T])
+        nc.sync.dma_start(pool[0][:, PREFIX:T], tok_planes[:, 0, PREFIX:T])
+        for t in (1, 2):
+            for lo, hi in ((0, PREFIX), (PREFIX, T)) if t in (1, 2) else ((0, T),):
+                nc.sync.dma_start(pool[t][:, lo:hi], tok_planes[:, t, lo:hi])
+        last_cuts = (0, PREFIX, T)
+        for lo, hi in zip(last_cuts, last_cuts[1:]):
+            nc.sync.dma_start(pool[3][:, lo:hi], tok_planes[:, 3, lo:hi])
         for h, (lo, hi) in enumerate(w_parts):
             nc.sync.dma_start(w_raw[h][:], wo_planes[:, :, lo:hi])
 
@@ -85,45 +96,52 @@ def tile_attend_shortconv_pl_kernel(tc, tok, fa, fb, fc, fe, wo, offs, out_0, ou
             return slice(c * CHUNK, (c + 1) * CHUNK)
 
         def gather(t, lo, hi):
-            window = pool[t][:, 0 : T - I + hi]
-            nc.vector.tensor_copy(shifted(t, 0, lo, hi), window.indirect(offsets[:, lo // 16 : hi // 16]))
-            nc.scalar.activation(terms[t][0][:, lo:hi], shifted(t, 2, lo, hi), COPY, scale=tap(2, t))
-            nc.scalar.activation(terms[t][1][:, lo:hi], shifted(t, 3, lo, hi), COPY, scale=tap(3, t))
-
-        def scale_own(t, lo, hi):
-            nc.vector.tensor_scalar(own[t][:, lo:hi], shifted(t, 0, lo, hi), tap(0, t), None, MULT)
-
-        def mix(t, lo, hi):
-            if t <= 1 or t == 3 and lo > 0:
-                nc.vector.tensor_scalar(terms[t][2][:, lo:hi], shifted(t, 1, lo, hi), tap(1, t), None, MULT)
+            listed = pool[t][:, 0 : max(PREFIX, T - I + hi)].indirect(offsets[:, lo // 16 : hi // 16])
+            if False:
+                nc.vector.tensor_copy(shifted(t, 0, lo, hi), listed)
             else:
-                nc.vector.scalar_tensor_tensor(terms[t][2][:, lo:hi], shifted(t, 1, lo, hi), tap(1, t), own[t][:, lo:hi], MULT, ADD)
+                nc.scalar.activation(shifted(t, 0, lo, hi), listed, COPY)
 
-        early = [psum.tile([P, 2, 2, P], F32, name=f"early{c}", tag=f"bank{CHUNKS + c}") for c in range(CHUNKS)]
-        late = [psum.tile([P, 2, P], F32, name=f"late{c}", tag=f"bank{c}") for c in range(CHUNKS)]
-        sums = [(early[c][:, 0, :, :], late[c][:]) for c in range(CHUNKS)]
-        back = [early[c][:, 1, :, :] for c in range(CHUNKS)]
-        pairs = [[keep.tile([P, P, 2], BF16, name=f"pairs{c}_{u}", align_bytes=64) for u in range(2)] for c in range(CHUNKS)]
+        def mix(t, h):
+            lo, hi = h * HALF, (h + 1) * HALF
+            for k in (2, 0, 1):
+                nc.vector.tensor_scalar(terms[t][h][k][:], shifted(t, k, lo, hi), tap(k, t), None, MULT)
+            last = terms[t][h][2][:]
+            nc.vector.scalar_tensor_tensor(last, shifted(t, 3, lo, hi), tap(3, t), last, MULT, ADD)
+
+        low_sums = [psum.tile([P, 2, 2, P], F32, name=f"low_sums{h}", tag=f"bank{CHUNKS + 2 * h}") for h in range(2)]
+        high_sums = [psum.tile([P, 2, P], F32, name=f"high_sums{c}", tag=f"bank{c}") for c in range(CHUNKS)]
+        back = [psum.tile([P, 2, P], F32, name=f"back{c}", tag=f"bank{CHUNKS + c}") for c in range(CHUNKS)]
+        sums = [(low_sums[c // 2][:, c % 2, :, :], high_sums[c][:]) for c in range(CHUNKS)]
+        low = [keep.tile([P, 2, P, 2], BF16, name="low0", align_bytes=64), keep.tile([P, 2, P, 2], BF16, name="low1", tag="pool2", align_bytes=64)]
+        high = [keep.tile([P, P, 2], BF16, name=f"high{c}", align_bytes=64) for c in range(CHUNKS - 1)]
+        high.append(shared.tile([P, P, 2], BF16, name="high_last", align_bytes=64, offset=4 * I))
 
         def add_terms(t, chunks):
-            lo = chunks[0] * CHUNK
-            parts = [own[t], terms[t][0], terms[t][2], terms[t][1]] if t <= 1 or t == 3 and lo > 0 else terms[t]
-            for k, part in enumerate(parts):
+            for k in range(TERMS):
                 for c in chunks:
                     nc.tensor.matmul(
-                        sums[c][t // 2][:, t % 2, :], part[:, slots(c)], ident[:], start=k == 0, stop=k == len(parts) - 1, is_transpose=True
+                        sums[c][t // 2][:, t % 2, :], terms[t][c // 2][k][:, slots(c % 2)], ident[:], start=k == 0, stop=k == TERMS - 1, is_transpose=True
                     )
 
-        def round_x(c, u):
-            nc.scalar.copy(pairs[c][u][:], sums[c][u].rearrange("i e p -> i p e"))
+        def turn_back(c, u, pairs):
+            nc.tensor.transpose(back[c][:, u, :], pairs.rearrange("i p e -> i (p e)").bitcast(F32), ident[:])
 
-        def turn_back(c, u):
-            words = pairs[c][u][:].rearrange("i p e -> i (p e)").bitcast(F32)
-            nc.tensor.transpose(back[c][:, u, :], words, ident[:])
+        def round_low(h):
+            copy = nc.vector.tensor_copy if h == 0 else nc.scalar.copy
+            copy(low[h][:], low_sums[h][:].rearrange("i c e p -> i c p e"))
+            for c in range(2):
+                turn_back(2 * h + c, 0, low[h][:, c, :, :])
+
+        def round_high(c):
+            copy = nc.vector.tensor_copy if c == 3 else nc.scalar.copy
+            copy(high[c][:], high_sums[c][:].rearrange("i e p -> i p e"))
+            turn_back(c, 1, high[c][:])
 
         def round_w(h):
             m = slice(w_parts[h][0] // PACK, w_parts[h][1] // PACK)
-            nc.vector.tensor_copy(
+            copy = nc.scalar.copy if h == 0 else nc.vector.tensor_copy
+            copy(
                 w_bf[:, :, m, :].rearrange("p r m t -> p m t r"),
                 w_raw[h][:].rearrange("p t (m r) -> p m t r", r=PACK),
             )
@@ -136,20 +154,13 @@ def tile_attend_shortconv_pl_kernel(tc, tok, fa, fb, fc, fe, wo, offs, out_0, ou
                 in_=w_bf[:, 2 * b : 2 * b + 2, :, :].rearrange("p r m t -> p (r m t)"),
             )
 
-        def runs(planes):
-            return planes.rearrange("p t (c i) -> p c t i", i=RUN)
-
-        x_codes = keep.tile([P, I], U32, name="x_codes", tag=f"w_raw{F}", align_bytes=64)
-        y_bf = keep.tile([P, I, PACK], BF16, name="y_bf", align_bytes=64)
-        y_all = keep.tile([P, PACK, I], F32, name="y_all", align_bytes=64)
-        y_sb = [y_all[:, :, slots(c)] for c in range(CHUNKS)]
-        x_bf, x_scales = [], []
-        for c in range(CHUNKS):
-            x_bf.append(keep.tile([P, CHUNK, 2], F32, name=f"x_bf{c}", align_bytes=64))
-            x_scales.append(keep.tile([P, CHUNK], U8, name=f"x_scales{c}", align_bytes=64))
+        x_codes = shared.tile([P, I], U32, name="x_codes", align_bytes=64, offset=0)
+        x_bf = [keep.tile([P, CHUNK, 2], F32, name=f"x_bf{c}", align_bytes=64) for c in range(CHUNKS)]
+        x_scales = [keep.tile([P, CHUNK], U8, name=f"x_scales{c}", align_bytes=64) for c in range(CHUNKS)]
 
         def weave_x(c):
-            nc.scalar.copy(x_bf[c][:], back[c].rearrange("p u i -> p i u"))
+            copy = nc.vector.tensor_copy if False else nc.scalar.copy
+            copy(x_bf[c][:], back[c][:].rearrange("p u i -> p i u"))
 
         def quantize_x(c):
             nc.vector.quantize_mx(
@@ -171,16 +182,17 @@ def tile_attend_shortconv_pl_kernel(tc, tok, fa, fb, fc, fe, wo, offs, out_0, ou
                     start=True,
                     stop=True,
                 )
-            nc.scalar.copy(y_sb[c][:, 2 * b : 2 * b + 2, :], acc[:])
+            copy = nc.vector.tensor_copy if False else nc.scalar.copy
+            copy(y_all[:, 2 * b : 2 * b + 2, slots(c)], acc[:])
 
         def store_y(b, lo, hi):
             nc.sync.dma_start(y_rows[:, 2 * b : 2 * b + 2, lo:hi], y_all[:, 2 * b : 2 * b + 2, lo:hi])
 
         def round_y(lo, hi):
-            c, at = divmod(lo, CHUNK)
             copy = nc.scalar.copy if hi == I else nc.vector.tensor_copy
             copy(
-                y_bf[:, lo:hi, :].rearrange("p (c i) r -> p c r i", i=RUN), runs(y_sb[c][:, :, at : at + hi - lo])
+                y_bf[:, lo:hi, :].rearrange("p (c i) r -> p c r i", i=RUN),
+                y_all[:, :, lo:hi].rearrange("p r (c i) -> p c r i", i=RUN),
             )
 
         def quantize_y(lo, hi):
@@ -191,25 +203,32 @@ def tile_attend_shortconv_pl_kernel(tc, tok, fa, fb, fc, fe, wo, offs, out_0, ou
             )
 
         for t in range(PACK):
-            for step in (gather, scale_own, mix):
-                step(t, 0, HALF)
-                step(t, HALF, I)
-            for chunks in ((0, 1), (2, 3)):
+            pieces = ((0, HALF), (HALF, I)) if t == PACK - 1 else ((0, HALF), (HALF, I))
+            for lo, hi in pieces:
+                gather(t, lo, hi)
+            for h in range(2):
+                mix(t, h)
+            for chunks in ((0,), (1,), (2,), (3,)) if t < 2 else ((0, 1), (2, 3)):
                 add_terms(t, chunks)
-            if t >= 2:
-                for step in (round_x, turn_back):
-                    for c in range(CHUNKS):
-                        step(c, t - 2)
+            if t == 1:
+                round_low(0)
+            if t == 2:
+                round_low(1)
+        for c in range(3):
+            round_high(c)
         for h in range(len(w_parts)):
             round_w(h)
-        for c in range(CHUNKS):
-            weave_x(c)
+        round_high(3)
+        weave_x(0)
+        weave_x(1)
         quantize_w(0)
         quantize_x(0)
+        quantize_x(1)
         quantize_w(1)
-        for c in range(1, CHUNKS):
+        for c in (2, 3):
+            weave_x(c)
             quantize_x(c)
-        banks = (3, 0, 4, 5, 1, 2, 6, 7)
+        banks = (0, 1, 4, 5, 2, 3, 6, 7)
         for h in range(2):
             for b in range(2):
                 for c in (2 * h, 2 * h + 1):

@@ -45,10 +45,10 @@ def tile_attend_shortconv_pl_kernel(tc, tok, fa, fb, fc, fe, wo, offs, out_0, ou
         offsets = keep.tile([P, I // 16], U16, name="offsets")
         pool = [keep.tile([P, T], F32, name=f"pool{t}", tag=f"pool{t}", align_bytes=64) for t in range(PACK)]
         taps = [keep.tile([P, PACK], F32, name=f"tap{k}") for k in range(TAPS)]
-        w_cuts = (0, F // 4, 11 * F // 16, F)
+        w_cuts = (0, 3 * F // 8, 3 * F // 4, F)
         w_parts = list(zip(w_cuts, w_cuts[1:]))
         w_raw = [keep.tile([P, PACK, hi - lo], F32, name=f"w_raw{lo}", align_bytes=64) for lo, hi in w_parts[:-1]]
-        w_raw.append(shared.tile([P, PACK, F - w_cuts[-2]], F32, name="w_last", align_bytes=64, offset=0))
+        w_raw.append(shared.tile([P, PACK, F - w_cuts[-2]], F32, name="w_last", align_bytes=64, offset=4 * I + 4 * P - 4 * PACK * (F - w_cuts[-2])))
         picked = [keep.tile([P, PAD + I], F32, name=f"picked{t}", align_bytes=64) for t in range(PACK)]
         terms = [
             [
@@ -146,12 +146,12 @@ def tile_attend_shortconv_pl_kernel(tc, tok, fa, fb, fc, fe, wo, offs, out_0, ou
                 w_raw[h][:].rearrange("p t (m r) -> p m t r", r=PACK),
             )
 
-        def quantize_w(b):
-            cols = slice(2 * b * P, 2 * (b + 1) * P)
+        def quantize_w(lo, hi):
+            cols = slice(lo * P, hi * P)
             nc.vector.quantize_mx(
                 out=w_codes[:, cols].bitcast(FP8X4),
                 scales=w_scales[:, cols],
-                in_=w_bf[:, 2 * b : 2 * b + 2, :, :].rearrange("p r m t -> p (r m t)"),
+                in_=w_bf[:, lo:hi, :, :].rearrange("p r m t -> p (r m t)"),
             )
 
         x_codes = shared.tile([P, I], U32, name="x_codes", align_bytes=64, offset=0)
@@ -182,7 +182,7 @@ def tile_attend_shortconv_pl_kernel(tc, tok, fa, fb, fc, fe, wo, offs, out_0, ou
                     start=True,
                     stop=True,
                 )
-            copy = nc.vector.tensor_copy if False else nc.scalar.copy
+            copy = nc.vector.tensor_copy if (c, b) == (0, 1) else nc.scalar.copy
             copy(y_all[:, 2 * b : 2 * b + 2, slots(c)], acc[:])
 
         def store_y(b, lo, hi):
@@ -221,10 +221,11 @@ def tile_attend_shortconv_pl_kernel(tc, tok, fa, fb, fc, fe, wo, offs, out_0, ou
         round_high(3)
         weave_x(0)
         weave_x(1)
-        quantize_w(0)
+        quantize_w(0, 1)
         quantize_x(0)
+        quantize_w(1, 2)
         quantize_x(1)
-        quantize_w(1)
+        quantize_w(2, 4)
         for c in (2, 3):
             weave_x(c)
             quantize_x(c)

@@ -102,11 +102,12 @@ def tile_attend_shortconv_pl_kernel(tc, tok, fa, fb, fc, fe, wo, offs, out_0, ou
             else:
                 nc.scalar.activation(shifted(t, 0, lo, hi), listed, COPY)
 
-        def mix(t, h):
-            lo, hi = h * HALF, (h + 1) * HALF
+        def mix(t, lo, hi):
+            h, at = divmod(lo, HALF)
+            cols = slice(at, at + hi - lo)
             for k in (2, 0, 1):
-                nc.vector.tensor_scalar(terms[t][h][k][:], shifted(t, k, lo, hi), tap(k, t), None, MULT)
-            last = terms[t][h][2][:]
+                nc.vector.tensor_scalar(terms[t][h][k][:, cols], shifted(t, k, lo, hi), tap(k, t), None, MULT)
+            last = terms[t][h][2][:, cols]
             nc.vector.scalar_tensor_tensor(last, shifted(t, 3, lo, hi), tap(3, t), last, MULT, ADD)
 
         low_sums = [psum.tile([P, 2, 2, P], F32, name=f"low_sums{h}", tag=f"bank{CHUNKS + 2 * h}") for h in range(2)]
@@ -182,7 +183,7 @@ def tile_attend_shortconv_pl_kernel(tc, tok, fa, fb, fc, fe, wo, offs, out_0, ou
                     start=True,
                     stop=True,
                 )
-            copy = nc.vector.tensor_copy if (c, b) == (0, 1) else nc.scalar.copy
+            copy = nc.vector.tensor_copy if b == 1 and c in (0, 2) else nc.scalar.copy
             copy(y_all[:, 2 * b : 2 * b + 2, slots(c)], acc[:])
 
         def store_y(b, lo, hi):
@@ -203,12 +204,12 @@ def tile_attend_shortconv_pl_kernel(tc, tok, fa, fb, fc, fe, wo, offs, out_0, ou
             )
 
         for t in range(PACK):
-            pieces = ((0, HALF), (HALF, I)) if t == PACK - 1 else ((0, HALF), (HALF, I))
+            pieces = ((0, CHUNK), (CHUNK, HALF), (HALF, I)) if t == PACK - 1 else ((0, HALF), (HALF, I))
             for lo, hi in pieces:
                 gather(t, lo, hi)
-            for h in range(2):
-                mix(t, h)
-            for chunks in ((0,), (1,), (2,), (3,)) if t < 2 else ((0, 1), (2, 3)):
+            for lo, hi in pieces:
+                mix(t, lo, hi)
+            for chunks in ((0,), (1,), (2,), (3,)) if t < 2 else ((0,), (1,), (2, 3)) if t == PACK - 1 else ((0, 1), (2, 3)):
                 add_terms(t, chunks)
             if t == 1:
                 round_low(0)
@@ -234,20 +235,19 @@ def tile_attend_shortconv_pl_kernel(tc, tok, fa, fb, fc, fe, wo, offs, out_0, ou
             for b in range(2):
                 for c in (2 * h, 2 * h + 1):
                     project(c, b, banks[4 * h + 2 * b + c % 2])
-                store_y(b, h * HALF, (h + 1) * HALF)
+                    if (h, b) == (0, 0):
+                        store_y(b, c * CHUNK, (c + 1) * CHUNK)
+                if (h, b) != (0, 0):
+                    store_y(b, h * HALF, (h + 1) * HALF)
         last = I - CHUNK
-        end = I - CHUNK // 2
         round_y(0, CHUNK)
         round_y(CHUNK, HALF)
-        round_y(HALF, last)
         quantize_y(0, HALF)
-        nc.sync.dma_start(words_out[:, 0:HALF], y_codes[:, 0:HALF].bitcast(I32))
-        round_y(last, end)
-        round_y(end, I)
+        round_y(HALF, last)
+        round_y(last, I)
         quantize_y(HALF, last)
-        quantize_y(last, end)
-        quantize_y(end, I)
-        nc.sync.dma_start(words_out[:, HALF:I], y_codes[:, HALF:I].bitcast(I32))
+        quantize_y(last, I)
+        nc.sync.dma_start(words_out, y_codes[:].bitcast(I32))
         for q in range(4):
             queue = nc.sync if q % 2 == 0 else nc.scalar
             queue.dma_start(scales_out[4 * q : 4 * q + 4, :], y_scales[32 * q : 32 * q + 4, :].bitcast(I32))

@@ -110,10 +110,10 @@ def tile_attend_shortconv_pl_kernel(tc, tok, fa, fb, fc, fe, wo, offs, out_0, ou
             last = terms[t][h][2][:, cols]
             nc.vector.scalar_tensor_tensor(last, shifted(t, 3, lo, hi), tap(3, t), last, MULT, ADD)
 
-        low_sums = [psum.tile([P, 2, 2, P], F32, name=f"low_sums{h}", tag=f"bank{CHUNKS + 2 * h}") for h in range(2)]
+        early = [psum.tile([P, 2, 2, P], F32, name=f"early{c}", tag=f"bank{CHUNKS + c}") for c in range(CHUNKS)]
         high_sums = [psum.tile([P, 2, P], F32, name=f"high_sums{c}", tag=f"bank{c}") for c in range(CHUNKS)]
-        back = [psum.tile([P, 2, P], F32, name=f"back{c}", tag=f"bank{CHUNKS + c}") for c in range(CHUNKS)]
-        sums = [(low_sums[c // 2][:, c % 2, :, :], high_sums[c][:]) for c in range(CHUNKS)]
+        back = [early[c][:, 1, :, :] for c in range(CHUNKS)]
+        sums = [(early[c][:, 0, :, :], high_sums[c][:]) for c in range(CHUNKS)]
         low = [keep.tile([P, 2, P, 2], BF16, name="low0", align_bytes=64), keep.tile([P, 2, P, 2], BF16, name="low1", tag="pool2", align_bytes=64)]
         high = [keep.tile([P, P, 2], BF16, name=f"high{c}", align_bytes=64) for c in range(CHUNKS - 1)]
         high.append(shared.tile([P, P, 2], BF16, name="high_last", align_bytes=64, offset=4 * I))
@@ -130,7 +130,8 @@ def tile_attend_shortconv_pl_kernel(tc, tok, fa, fb, fc, fe, wo, offs, out_0, ou
 
         def round_low(h):
             copy = nc.vector.tensor_copy if h == 0 else nc.scalar.copy
-            copy(low[h][:], low_sums[h][:].rearrange("i c e p -> i c p e"))
+            for c in range(2):
+                copy(low[h][:, c, :, :], sums[2 * h + c][0].rearrange("i e p -> i p e"))
             for c in range(2):
                 turn_back(2 * h + c, 0, low[h][:, c, :, :])
 
@@ -161,7 +162,7 @@ def tile_attend_shortconv_pl_kernel(tc, tok, fa, fb, fc, fe, wo, offs, out_0, ou
 
         def weave_x(c):
             copy = nc.vector.tensor_copy if False else nc.scalar.copy
-            copy(x_bf[c][:], back[c][:].rearrange("p u i -> p i u"))
+            copy(x_bf[c][:], back[c].rearrange("p u i -> p i u"))
 
         def quantize_x(c):
             nc.vector.quantize_mx(
@@ -209,7 +210,7 @@ def tile_attend_shortconv_pl_kernel(tc, tok, fa, fb, fc, fe, wo, offs, out_0, ou
                 gather(t, lo, hi)
             for lo, hi in pieces:
                 mix(t, lo, hi)
-            for chunks in ((0,), (1,), (2,), (3,)) if t < 2 else ((0,), (1,), (2, 3)) if t == PACK - 1 else ((0, 1), (2, 3)):
+            for chunks in ((0,), (1,), (2, 3)) if t == PACK - 1 else ((0, 1), (2, 3)):
                 add_terms(t, chunks)
             if t == 1:
                 round_low(0)

@@ -52,7 +52,7 @@ def tile_attend_shortconv_pl_kernel(tc, tok, fa, fb, fc, fe, wo, offs, out_0, ou
         picked = [keep.tile([P, PAD + I], F32, name=f"picked{t}", align_bytes=64) for t in range(PACK)]
         terms = [
             [
-                [keep.tile([P, HALF], F32, name=f"term{t}_{h}_{k}", tag=f"term{1 if (t, h) == (2, 0) else t}_{h}_{k}", align_bytes=64) for k in range(TERMS)]
+                [keep.tile([P, HALF], F32, name=f"term{t}_{h}_{k}", tag=f"term{1 if (t, h) == (2, 0) else t}_{h}_{k}", align_bytes=64) for k in range(4 if (t, h) == (3, 1) else 3)]
                 for h in range(2)
             ]
             for t in range(PACK)
@@ -69,7 +69,7 @@ def tile_attend_shortconv_pl_kernel(tc, tok, fa, fb, fc, fe, wo, offs, out_0, ou
 
         nc.sync.dma_start(pool[0][:, 0:PREFIX], tok_planes[:, 0, 0:PREFIX])
         nc.sync.dma_start(offsets[:], offs)
-        for k, factor in ((2, fc), (0, fa), (1, fb), (3, fe)):
+        for k, factor in ((2, fc), (1, fb), (0, fa), (3, fe)):
             nc.sync.dma_start(taps[k][:], factor.rearrange("(p t) o -> p (t o)", t=PACK))
         nc.sync.dma_start(pool[0][:, PREFIX:T], tok_planes[:, 0, PREFIX:T])
         for t in (1, 2):
@@ -105,10 +105,12 @@ def tile_attend_shortconv_pl_kernel(tc, tok, fa, fb, fc, fe, wo, offs, out_0, ou
         def mix(t, lo, hi):
             h, at = divmod(lo, HALF)
             cols = slice(at, at + hi - lo)
-            for k in (2, 0, 1):
+            count = len(terms[t][h])
+            for k in reversed(range(count)):
                 nc.vector.tensor_scalar(terms[t][h][k][:, cols], shifted(t, k, lo, hi), tap(k, t), None, MULT)
-            last = terms[t][h][2][:, cols]
-            nc.vector.scalar_tensor_tensor(last, shifted(t, 3, lo, hi), tap(3, t), last, MULT, ADD)
+            for k in reversed(range(count, TAPS)):
+                onto = terms[t][h][k - (TAPS - count)][:, cols]
+                nc.vector.scalar_tensor_tensor(onto, shifted(t, k, lo, hi), tap(k, t), onto, MULT, ADD)
 
         early = [psum.tile([P, 2, 2, P], F32, name=f"early{c}", tag=f"bank{CHUNKS + c}") for c in range(CHUNKS)]
         high_sums = [psum.tile([P, 2, P], F32, name=f"high_sums{c}", tag=f"bank{c}") for c in range(CHUNKS)]
@@ -118,11 +120,14 @@ def tile_attend_shortconv_pl_kernel(tc, tok, fa, fb, fc, fe, wo, offs, out_0, ou
         high = [keep.tile([P, P, 2], BF16, name=f"high{c}", align_bytes=64) for c in range(CHUNKS - 1)]
         high.append(shared.tile([P, P, 2], BF16, name="high_last", align_bytes=64, offset=4 * I))
 
+        sum_order = {2: (1, 0), 3: (1, 0, 2), 4: (3, 2, 1, 0)}
+
         def add_terms(t, chunks):
-            for k in range(TERMS):
+            count = len(terms[t][chunks[0] // 2])
+            for k in sum_order[count]:
                 for c in chunks:
                     nc.tensor.matmul(
-                        sums[c][t // 2][:, t % 2, :], terms[t][c // 2][k][:, slots(c % 2)], ident[:], start=k == 0, stop=k == TERMS - 1, is_transpose=True
+                        sums[c][t // 2][:, t % 2, :], terms[t][c // 2][k][:, slots(c % 2)], ident[:], start=k == sum_order[count][0], stop=k == sum_order[count][-1], is_transpose=True
                     )
 
         def turn_back(c, u, pairs):

@@ -20,12 +20,12 @@ COPY = mybir.ActivationFunctionType.Copy
 P = 128
 PACK = 4
 TAPS = 4
-TERMS = 3
 PAD = 8
 HALF = I // 2
 CHUNK = 128
 CHUNKS = I // CHUNK
 RUN = 4
+TAIL = 64
 PREFIX = T - HALF
 
 
@@ -72,12 +72,9 @@ def tile_attend_shortconv_pl_kernel(tc, tok, fa, fb, fc, fe, wo, offs, out_0, ou
         for k, factor in ((2, fc), (1, fb), (0, fa), (3, fe)):
             nc.sync.dma_start(taps[k][:], factor.rearrange("(p t) o -> p (t o)", t=PACK))
         nc.sync.dma_start(pool[0][:, PREFIX:T], tok_planes[:, 0, PREFIX:T])
-        for t in (1, 2):
-            for lo, hi in ((0, PREFIX), (PREFIX, T)) if t in (1, 2) else ((0, T),):
+        for t in range(1, PACK):
+            for lo, hi in ((0, PREFIX), (PREFIX, T)):
                 nc.sync.dma_start(pool[t][:, lo:hi], tok_planes[:, t, lo:hi])
-        last_cuts = (0, PREFIX, T)
-        for lo, hi in zip(last_cuts, last_cuts[1:]):
-            nc.sync.dma_start(pool[3][:, lo:hi], tok_planes[:, 3, lo:hi])
         for h, (lo, hi) in enumerate(w_parts):
             nc.sync.dma_start(w_raw[h][:], wo_planes[:, :, lo:hi])
 
@@ -97,10 +94,7 @@ def tile_attend_shortconv_pl_kernel(tc, tok, fa, fb, fc, fe, wo, offs, out_0, ou
 
         def gather(t, lo, hi):
             listed = pool[t][:, 0 : max(PREFIX, T - I + hi)].indirect(offsets[:, lo // 16 : hi // 16])
-            if False:
-                nc.vector.tensor_copy(shifted(t, 0, lo, hi), listed)
-            else:
-                nc.scalar.activation(shifted(t, 0, lo, hi), listed, COPY)
+            nc.scalar.activation(shifted(t, 0, lo, hi), listed, COPY)
 
         def mix(t, lo, hi):
             h, at = divmod(lo, HALF)
@@ -166,8 +160,7 @@ def tile_attend_shortconv_pl_kernel(tc, tok, fa, fb, fc, fe, wo, offs, out_0, ou
         x_scales = [keep.tile([P, CHUNK], U8, name=f"x_scales{c}", align_bytes=64) for c in range(CHUNKS)]
 
         def weave_x(c):
-            copy = nc.vector.tensor_copy if False else nc.scalar.copy
-            copy(x_bf[c][:], back[c].rearrange("p u i -> p i u"))
+            nc.scalar.copy(x_bf[c][:], back[c].rearrange("p u i -> p i u"))
 
         def quantize_x(c):
             nc.vector.quantize_mx(
@@ -176,27 +169,28 @@ def tile_attend_shortconv_pl_kernel(tc, tok, fa, fb, fc, fe, wo, offs, out_0, ou
                 in_=x_bf[c][:].rearrange("p i u -> p (i u)").bitcast(BF16),
             )
 
-        def project(c, b, bank):
-            acc = psum.tile([P, 2, CHUNK], F32, name=f"acc{c}_{b}", tag=f"bank{bank}")
+        def project(c, b, bank, lo=0, hi=CHUNK):
+            acc = psum.tile([P, 2, hi - lo], F32, name=f"acc{c}_{b}_{lo}", tag=f"bank{bank}")
+            mine = slice(c * CHUNK + lo, c * CHUNK + hi)
             for j in range(2):
                 cols = slice((2 * b + j) * P, (2 * b + j + 1) * P)
                 nc.tensor.matmul_mx(
                     out=acc[:, j, :],
                     lhsT=w_codes[:, cols].bitcast(FP8X4),
                     lhsT_scale=w_scales[:, cols],
-                    rhs=x_codes[:, slots(c)].bitcast(FP8X4),
-                    rhs_scale=x_scales[c][:],
+                    rhs=x_codes[:, mine].bitcast(FP8X4),
+                    rhs_scale=x_scales[c][:, lo:hi],
                     start=True,
                     stop=True,
                 )
-            copy = nc.vector.tensor_copy if b == 1 and c in (0, 2) else nc.scalar.copy
-            copy(y_all[:, 2 * b : 2 * b + 2, slots(c)], acc[:])
+            copy = nc.vector.tensor_copy if (b, c) in ((1, 0), (0, 2)) else nc.scalar.copy
+            copy(y_all[:, 2 * b : 2 * b + 2, mine], acc[:])
 
         def store_y(b, lo, hi):
             nc.sync.dma_start(y_rows[:, 2 * b : 2 * b + 2, lo:hi], y_all[:, 2 * b : 2 * b + 2, lo:hi])
 
         def round_y(lo, hi):
-            copy = nc.scalar.copy if hi == I else nc.vector.tensor_copy
+            copy = nc.scalar.copy if lo >= I - CHUNK else nc.vector.tensor_copy
             copy(
                 y_bf[:, lo:hi, :].rearrange("p (c i) r -> p c r i", i=RUN),
                 y_all[:, :, lo:hi].rearrange("p r (c i) -> p c r i", i=RUN),
@@ -240,7 +234,11 @@ def tile_attend_shortconv_pl_kernel(tc, tok, fa, fb, fc, fe, wo, offs, out_0, ou
         for h in range(2):
             for b in range(2):
                 for c in (2 * h, 2 * h + 1):
-                    project(c, b, banks[4 * h + 2 * b + c % 2])
+                    if (c, b) == (CHUNKS - 1, 1):
+                        project(c, b, banks[-1], 0, TAIL)
+                        project(c, b, banks[0], TAIL, CHUNK)
+                    else:
+                        project(c, b, banks[4 * h + 2 * b + c % 2])
                     if (h, b) == (0, 0):
                         store_y(b, c * CHUNK, (c + 1) * CHUNK)
                 if (h, b) != (0, 0):
@@ -248,11 +246,14 @@ def tile_attend_shortconv_pl_kernel(tc, tok, fa, fb, fc, fe, wo, offs, out_0, ou
         last = I - CHUNK
         round_y(0, CHUNK)
         round_y(CHUNK, HALF)
-        quantize_y(0, HALF)
+        quantize_y(0, CHUNK)
+        quantize_y(CHUNK, HALF)
         round_y(HALF, last)
-        round_y(last, I)
+        round_y(last, last + TAIL)
+        round_y(last + TAIL, I)
         quantize_y(HALF, last)
-        quantize_y(last, I)
+        quantize_y(last, last + TAIL)
+        quantize_y(last + TAIL, I)
         nc.sync.dma_start(words_out, y_codes[:].bitcast(I32))
         for q in range(4):
             queue = nc.sync if q % 2 == 0 else nc.scalar

@@ -186,8 +186,8 @@ def tile_attend_shortconv_pl_kernel(tc, tok, fa, fb, fc, fe, wo, offs, out_0, ou
             copy = nc.vector.tensor_copy if (b, c) in ((1, 0), (0, 2)) else nc.scalar.copy
             copy(y_all[:, 2 * b : 2 * b + 2, mine], acc[:])
 
-        def store_y(b, lo, hi):
-            nc.sync.dma_start(y_rows[:, 2 * b : 2 * b + 2, lo:hi], y_all[:, 2 * b : 2 * b + 2, lo:hi])
+        def store_y(first, end, lo, hi):
+            nc.sync.dma_start(y_rows[:, first:end, lo:hi], y_all[:, first:end, lo:hi])
 
         def round_y(lo, hi):
             copy = nc.scalar.copy if lo >= I - CHUNK else nc.vector.tensor_copy
@@ -239,10 +239,9 @@ def tile_attend_shortconv_pl_kernel(tc, tok, fa, fb, fc, fe, wo, offs, out_0, ou
                         project(c, b, banks[0], TAIL, CHUNK)
                     else:
                         project(c, b, banks[4 * h + 2 * b + c % 2])
-                    if (h, b) == (0, 0):
-                        store_y(b, c * CHUNK, (c + 1) * CHUNK)
-                if (h, b) != (0, 0):
-                    store_y(b, h * HALF, (h + 1) * HALF)
+                if h == 0:
+                    store_y(2 * b, 2 * b + 2, 0, HALF)
+        store_y(0, PACK, HALF, I)
         last = I - CHUNK
         round_y(0, CHUNK)
         round_y(CHUNK, HALF)

@@ -25,7 +25,6 @@ HALF = I // 2
 CHUNK = 128
 CHUNKS = I // CHUNK
 RUN = 4
-TAIL = 64
 PREFIX = T - HALF
 
 
@@ -169,22 +168,21 @@ def tile_attend_shortconv_pl_kernel(tc, tok, fa, fb, fc, fe, wo, offs, out_0, ou
                 in_=x_bf[c][:].rearrange("p i u -> p (i u)").bitcast(BF16),
             )
 
-        def project(c, b, bank, lo=0, hi=CHUNK):
-            acc = psum.tile([P, 2, hi - lo], F32, name=f"acc{c}_{b}_{lo}", tag=f"bank{bank}")
-            mine = slice(c * CHUNK + lo, c * CHUNK + hi)
+        def project(c, b, bank):
+            acc = psum.tile([P, 2, CHUNK], F32, name=f"acc{c}_{b}", tag=f"bank{bank}")
             for j in range(2):
                 cols = slice((2 * b + j) * P, (2 * b + j + 1) * P)
                 nc.tensor.matmul_mx(
                     out=acc[:, j, :],
                     lhsT=w_codes[:, cols].bitcast(FP8X4),
                     lhsT_scale=w_scales[:, cols],
-                    rhs=x_codes[:, mine].bitcast(FP8X4),
-                    rhs_scale=x_scales[c][:, lo:hi],
+                    rhs=x_codes[:, slots(c)].bitcast(FP8X4),
+                    rhs_scale=x_scales[c][:],
                     start=True,
                     stop=True,
                 )
             copy = nc.vector.tensor_copy if (b, c) in ((1, 0), (0, 2)) else nc.scalar.copy
-            copy(y_all[:, 2 * b : 2 * b + 2, mine], acc[:])
+            copy(y_all[:, 2 * b : 2 * b + 2, slots(c)], acc[:])
 
         def store_y(first, end, lo, hi):
             nc.sync.dma_start(y_rows[:, first:end, lo:hi], y_all[:, first:end, lo:hi])
@@ -234,11 +232,7 @@ def tile_attend_shortconv_pl_kernel(tc, tok, fa, fb, fc, fe, wo, offs, out_0, ou
         for h in range(2):
             for b in range(2):
                 for c in (2 * h, 2 * h + 1):
-                    if (c, b) == (CHUNKS - 1, 1):
-                        project(c, b, banks[-1], 0, TAIL)
-                        project(c, b, banks[0], TAIL, CHUNK)
-                    else:
-                        project(c, b, banks[4 * h + 2 * b + c % 2])
+                    project(c, b, banks[4 * h + 2 * b + c % 2])
                 if h == 0:
                     store_y(2 * b, 2 * b + 2, 0, HALF)
         store_y(0, PACK, HALF, I)
@@ -248,11 +242,9 @@ def tile_attend_shortconv_pl_kernel(tc, tok, fa, fb, fc, fe, wo, offs, out_0, ou
         quantize_y(0, CHUNK)
         quantize_y(CHUNK, HALF)
         round_y(HALF, last)
-        round_y(last, last + TAIL)
-        round_y(last + TAIL, I)
+        round_y(last, I)
         quantize_y(HALF, last)
-        quantize_y(last, last + TAIL)
-        quantize_y(last + TAIL, I)
+        quantize_y(last, I)
         nc.sync.dma_start(words_out, y_codes[:].bitcast(I32))
         for q in range(4):
             queue = nc.sync if q % 2 == 0 else nc.scalar

from contextlib import ExitStack

import concourse.mybir as mybir
from concourse.masks import make_identity

D, T, I, F = 512, 2048, 512, 512
FLOPS = 2 * D * F * I

F32 = mybir.dt.float32
BF16 = mybir.dt.bfloat16
I32 = mybir.dt.int32
U32 = mybir.dt.uint32
U16 = mybir.dt.uint16
U8 = mybir.dt.uint8
FP8X4 = mybir.dt.float8_e4m3fn_x4
MULT = mybir.AluOpType.mult
ADD = mybir.AluOpType.add
COPY = mybir.ActivationFunctionType.Copy

P = 128
PACK = 4
TAPS = 4
PAD = 8
HALF = I // 2
CHUNK = 128
CHUNKS = I // CHUNK
RUN = 4
PREFIX = T - HALF


def tile_attend_shortconv_pl_kernel(tc, tok, fa, fb, fc, fe, wo, offs, out_0, out_1, out_2):
    nc = tc.nc
    tok_planes = tok.rearrange("(p t) n -> p t n", t=PACK)
    wo_planes = wo.rearrange("(p t) f -> p t f", t=PACK)
    y_rows = out_0.rearrange("(p r) i -> p r i", r=PACK)
    words_out = out_1[0].rearrange("p c r -> p (c r)").bitcast(I32)
    scales_out = out_2[0].bitcast(I32)

    with ExitStack() as ctx:
        keep = ctx.enter_context(tc.tile_pool(name="keep", bufs=1))
        shared = ctx.enter_context(tc.tile_pool(name="shared", bufs=1))
        psum = ctx.enter_context(tc.psum_pool(name="psum", bufs=1))

        offsets = keep.tile([P, I // 16], U16, name="offsets")
        pool = [keep.tile([P, T], F32, name=f"pool{t}", tag=f"pool{t}", align_bytes=64) for t in range(PACK)]
        taps = [keep.tile([P, PACK], F32, name=f"tap{k}") for k in range(TAPS)]
        w_cuts = (0, 3 * F // 8, 3 * F // 4, F)
        w_parts = list(zip(w_cuts, w_cuts[1:]))
        w_raw = [keep.tile([P, PACK, hi - lo], F32, name=f"w_raw{lo}", align_bytes=64) for lo, hi in w_parts[:-1]]
        w_raw.append(shared.tile([P, PACK, F - w_cuts[-2]], F32, name="w_last", align_bytes=64, offset=4 * I + 4 * P - 4 * PACK * (F - w_cuts[-2])))
        picked = [keep.tile([P, PAD + I], F32, name=f"picked{t}", align_bytes=64) for t in range(PACK)]
        terms = [
            [
                [keep.tile([P, HALF], F32, name=f"term{t}_{h}_{k}", tag=f"term{1 if (t, h) == (2, 0) else t}_{h}_{k}", align_bytes=64) for k in range(4 if (t, h) == (3, 1) else 3)]
                for h in range(2)
            ]
            for t in range(PACK)
        ]
        zeros = keep.tile([P, PAD], F32, name="zeros")
        ident = keep.tile([P, P], F32, name="ident", align_bytes=64)
        w_bf = keep.tile([P, PACK, P, PACK], BF16, name="w_bf", align_bytes=64)
        w_codes = keep.tile([P, F], U32, name="w_codes", align_bytes=64)
        w_scales = keep.tile([P, F], U8, name="w_scales", align_bytes=64)
        y_all = keep.tile([P, PACK, I], F32, name="y_all", align_bytes=64)
        y_bf = keep.tile([P, I, PACK], BF16, name="y_bf", align_bytes=64)
        y_codes = keep.tile([P, I], U32, name="y_codes", align_bytes=64)
        y_scales = keep.tile([P, I], U8, name="y_scales", align_bytes=64)

        nc.sync.dma_start(pool[0][:, 0:PREFIX], tok_planes[:, 0, 0:PREFIX])
        nc.sync.dma_start(offsets[:], offs)
        for k, factor in ((2, fc), (1, fb), (0, fa), (3, fe)):
            nc.sync.dma_start(taps[k][:], factor.rearrange("(p t) o -> p (t o)", t=PACK))
        nc.sync.dma_start(pool[0][:, PREFIX:T], tok_planes[:, 0, PREFIX:T])
        for t in range(1, PACK):
            for lo, hi in ((0, PREFIX), (PREFIX, T)):
                nc.sync.dma_start(pool[t][:, lo:hi], tok_planes[:, t, lo:hi])
        for h, (lo, hi) in enumerate(w_parts):
            nc.sync.dma_start(w_raw[h][:], wo_planes[:, :, lo:hi])

        nc.vector.memset(zeros[:], 0.0)
        for t in range(PACK):
            nc.scalar.activation(picked[t][:, 0:PAD], zeros[:], COPY)
        make_identity(nc, ident[:])

        def shifted(t, k, lo, hi):
            return picked[t][:, PAD + lo - k : PAD + hi - k]

        def tap(k, t):
            return taps[k][:, t : t + 1]

        def slots(c):
            return slice(c * CHUNK, (c + 1) * CHUNK)

        def gather(t, lo, hi):
            listed = pool[t][:, 0 : max(PREFIX, T - I + hi)].indirect(offsets[:, lo // 16 : hi // 16])
            nc.scalar.activation(shifted(t, 0, lo, hi), listed, COPY)

        def mix(t, lo, hi):
            h, at = divmod(lo, HALF)
            cols = slice(at, at + hi - lo)
            count = len(terms[t][h])
            for k in reversed(range(count)):
                nc.vector.tensor_scalar(terms[t][h][k][:, cols], shifted(t, k, lo, hi), tap(k, t), None, MULT)
            for k in reversed(range(count, TAPS)):
                onto = terms[t][h][k - (TAPS - count)][:, cols]
                nc.vector.scalar_tensor_tensor(onto, shifted(t, k, lo, hi), tap(k, t), onto, MULT, ADD)

        early = [psum.tile([P, 2, 2, P], F32, name=f"early{c}", tag=f"bank{CHUNKS + c}") for c in range(CHUNKS)]
        high_sums = [psum.tile([P, 2, P], F32, name=f"high_sums{c}", tag=f"bank{c}") for c in range(CHUNKS)]
        back = [early[c][:, 1, :, :] for c in range(CHUNKS)]
        sums = [(early[c][:, 0, :, :], high_sums[c][:]) for c in range(CHUNKS)]
        low = [keep.tile([P, 2, P, 2], BF16, name="low0", align_bytes=64), keep.tile([P, 2, P, 2], BF16, name="low1", tag="pool2", align_bytes=64)]
        high = [keep.tile([P, P, 2], BF16, name=f"high{c}", align_bytes=64) for c in range(CHUNKS - 1)]
        high.append(shared.tile([P, P, 2], BF16, name="high_last", align_bytes=64, offset=4 * I))

        sum_order = {2: (1, 0), 3: (1, 0, 2), 4: (3, 2, 1, 0)}

        def add_terms(t, chunks):
            count = len(terms[t][chunks[0] // 2])
            for k in sum_order[count]:
                for c in chunks:
                    nc.tensor.matmul(
                        sums[c][t // 2][:, t % 2, :], terms[t][c // 2][k][:, slots(c % 2)], ident[:], start=k == sum_order[count][0], stop=k == sum_order[count][-1], is_transpose=True
                    )

        def turn_back(c, u, pairs):
            nc.tensor.transpose(back[c][:, u, :], pairs.rearrange("i p e -> i (p e)").bitcast(F32), ident[:])

        def round_low(h):
            copy = nc.vector.tensor_copy if h == 0 else nc.scalar.copy
            for c in range(2):
                copy(low[h][:, c, :, :], sums[2 * h + c][0].rearrange("i e p -> i p e"))
            for c in range(2):
                turn_back(2 * h + c, 0, low[h][:, c, :, :])

        def round_high(c):
            copy = nc.vector.tensor_copy if c == 3 else nc.scalar.copy
            copy(high[c][:], high_sums[c][:].rearrange("i e p -> i p e"))
            turn_back(c, 1, high[c][:])

        def round_w(h):
            m = slice(w_parts[h][0] // PACK, w_parts[h][1] // PACK)
            copy = nc.scalar.copy if h == 0 else nc.vector.tensor_copy
            copy(
                w_bf[:, :, m, :].rearrange("p r m t -> p m t r"),
                w_raw[h][:].rearrange("p t (m r) -> p m t r", r=PACK),
            )

        def quantize_w(lo, hi):
            cols = slice(lo * P, hi * P)
            nc.vector.quantize_mx(
                out=w_codes[:, cols].bitcast(FP8X4),
                scales=w_scales[:, cols],
                in_=w_bf[:, lo:hi, :, :].rearrange("p r m t -> p (r m t)"),
            )

        x_codes = shared.tile([P, I], U32, name="x_codes", align_bytes=64, offset=0)
        x_bf = [keep.tile([P, CHUNK, 2], F32, name=f"x_bf{c}", align_bytes=64) for c in range(CHUNKS)]
        x_scales = [keep.tile([P, CHUNK], U8, name=f"x_scales{c}", align_bytes=64) for c in range(CHUNKS)]

        def weave_x(c):
            nc.scalar.copy(x_bf[c][:], back[c].rearrange("p u i -> p i u"))

        def quantize_x(c):
            nc.vector.quantize_mx(
                out=x_codes[:, slots(c)].bitcast(FP8X4),
                scales=x_scales[c][:],
                in_=x_bf[c][:].rearrange("p i u -> p (i u)").bitcast(BF16),
            )

        def project(c, b, bank):
            acc = psum.tile([P, 2, CHUNK], F32, name=f"acc{c}_{b}", tag=f"bank{bank}")
            for j in range(2):
                cols = slice((2 * b + j) * P, (2 * b + j + 1) * P)
                nc.tensor.matmul_mx(
                    out=acc[:, j, :],
                    lhsT=w_codes[:, cols].bitcast(FP8X4),
                    lhsT_scale=w_scales[:, cols],
                    rhs=x_codes[:, slots(c)].bitcast(FP8X4),
                    rhs_scale=x_scales[c][:],
                    start=True,
                    stop=True,
                )
            copy = nc.vector.tensor_copy if (b, c) in ((1, 0), (0, 2)) else nc.scalar.copy
            copy(y_all[:, 2 * b : 2 * b + 2, slots(c)], acc[:])

        def store_y(first, end, lo, hi):
            nc.sync.dma_start(y_rows[:, first:end, lo:hi], y_all[:, first:end, lo:hi])

        def round_y(lo, hi):
            copy = nc.scalar.copy if lo >= I - CHUNK else nc.vector.tensor_copy
            copy(
                y_bf[:, lo:hi, :].rearrange("p (c i) r -> p c r i", i=RUN),
                y_all[:, :, lo:hi].rearrange("p r (c i) -> p c r i", i=RUN),
            )

        def quantize_y(lo, hi):
            nc.vector.quantize_mx(
                out=y_codes[:, lo:hi].bitcast(FP8X4),
                scales=y_scales[:, lo:hi],
                in_=y_bf[:, lo:hi, :].rearrange("p i r -> p (i r)"),
            )

        for t in range(PACK):
            pieces = ((0, CHUNK), (CHUNK, HALF), (HALF, I)) if t == PACK - 1 else ((0, HALF), (HALF, I))
            for lo, hi in pieces:
                gather(t, lo, hi)
            for lo, hi in pieces:
                mix(t, lo, hi)
            for chunks in ((0,), (1,), (2, 3)) if t == PACK - 1 else ((0, 1), (2, 3)):
                add_terms(t, chunks)
            if t == 1:
                round_low(0)
            if t == 2:
                round_low(1)
        for c in range(3):
            round_high(c)
        for h in range(len(w_parts)):
            round_w(h)
        round_high(3)
        weave_x(0)
        weave_x(1)
        quantize_w(0, 1)
        quantize_x(0)
        quantize_w(1, 2)
        quantize_x(1)
        quantize_w(2, 4)
        for c in (2, 3):
            weave_x(c)
            quantize_x(c)
        banks = (0, 1, 4, 5, 2, 3, 6, 7)
        for h in range(2):
            for b in range(2):
                for c in (2 * h, 2 * h + 1):
                    project(c, b, banks[4 * h + 2 * b + c % 2])
                if h == 0:
                    store_y(2 * b, 2 * b + 2, 0, HALF)
        store_y(0, PACK, HALF, I)
        last = I - CHUNK
        round_y(0, CHUNK)
        round_y(CHUNK, HALF)
        quantize_y(0, CHUNK)
        quantize_y(CHUNK, HALF)
        round_y(HALF, last)
        round_y(last, I)
        quantize_y(HALF, last)
        quantize_y(last, I)
        nc.sync.dma_start(words_out, y_codes[:].bitcast(I32))
        for q in range(4):
            queue = nc.sync if q % 2 == 0 else nc.scalar
            queue.dma_start(scales_out[4 * q : 4 * q + 4, :], y_scales[32 * q : 32 * q + 4, :].bitcast(I32))
